import numpy as np, ml_dtypes
CORES = [3,7,11,15,131,135,139,143]
N = 8
BF = ml_dtypes.bfloat16
V, L, K, RO, KM = 2048, 256, 16, 3, 3967
B = L // N
WT = np.array([1, 7, 2, 6, 3, 5, 4, 4, 5, 3, 6, 2, 7, 1, 8, 1], np.int64)
def mix(v):
    return np.add.reduce(v * WT[:, None], axis=-2)
def spots(u, kap, a):
    return ((u * u >> 5)[..., None, :] + kap[..., None] * u[..., None, :] + a[..., None, None]) & (V - 1)
def first(x, z, kap, a=0):
    h = spots(mix(z), kap, np.asarray(a, np.int64)); e = np.add.reduce(np.abs(x[:, h] - z[:, None, :]), axis=0); m = np.argmin(e, axis=0)[None]
    return np.take_along_axis(h, m, 0)[0], np.take_along_axis(e, m, 0)[0]
def back(x, t, s):
    node = t[np.maximum(np.argsort(t)[s] - 1 - (1 + (mix(x[:, s]) & 15)) * np.arange(K)[:, None], 0)]
    e = np.add.reduce(np.abs(x[:, node] - x[:, None, s]), axis=0)
    return np.take_along_axis(node, np.argmin(e, axis=0)[None], 0)[0]
def far(rng):
    q = int(rng.integers(80, 113)); a = q // 2 + rng.integers(-7, 8, (8, L)); z = np.concatenate([a, q - a]); z[0] -= rng.integers(0, 4, L)
    return rng.integers(0, 8, (16, V)), z
def apart(rng, kap):
    z = rng.integers(2, 62, (16, L)); z[0] ^= 1 - (mix(z) & 1)
    h = spots(mix(z), kap, np.zeros((), np.int64)); used = np.zeros(V, bool); s = np.zeros(L, np.int64)
    for l in range(L):
        c = h[:, l]; s[l] = c[int(np.argmin(used[c]))]; used[s[l]] = True
    us, i = np.unique(s, return_index=True); k = len(us); rest = rng.permutation(np.flatnonzero(~used)); n = rest[:k]; rest = rest[k:]
    x = rng.integers(0, 64, (16, V)); x[:, us] = z[:, i] + rng.integers(-1, 2, (16, k)); x[:, n] = z[:, i] + 4 * rng.integers(0, 2, (16, k)) - 2
    o = rng.permutation(k); j = int(rng.integers(0, len(rest) // 2)); two = np.stack([n[o], us[o]], axis=1).reshape(-1)
    return x, z, np.concatenate([rest[:j], two, rest[j:]])
def parts(rng):
    x = rng.integers(0, 64, (N, 8, 16, V)); z = rng.integers(0, 64, (N, 8, 16, L)); ts = np.argsort(rng.random((N, 8, V)), axis=-1)
    return x, z, ts, rng.integers(0, KM + 1, (N, 8, 16)), rng.integers(20, 261, (N, 8))
def pack(x, z, ts, kap, th):
    return {"xr": np.ascontiguousarray(x.reshape(N, 128, V)).astype(np.float32).astype(BF), "ts": np.ascontiguousarray(ts).astype(np.int32), "zq": np.ascontiguousarray(z.reshape(N, 128, L)).astype(np.float32).astype(BF),
            "kap": np.ascontiguousarray(kap.reshape(N, 128, 1)).astype(np.int32), "th": np.ascontiguousarray(th.reshape(N, 8, 1)).astype(np.int32)}
def plant(rng, x, z, kap):
    h = spots(mix(z), kap, np.zeros((N, 8), np.int64)); m = rng.integers(0, 16, (N, 8, 1, L)); h = np.take_along_axis(h, m, 2)[:, :, 0]
    for r in range(N):
        for g in range(8):
            w = np.flatnonzero(rng.random(L) < rng.choice(np.array([0.2, 0.4, 0.6]))); c = int(rng.integers(2, 14))
            x[r, g][:, h[r, g, w]] = np.clip(z[r, g][:, w] + rng.integers(-c, c + 1, (16, len(w))), 0, 63)
def setup_inputs(rng):
    x, z, ts, kap, th = parts(rng)
    src = np.where(rng.random((N, 8, L)) < 0.12, rng.integers(0, L, (N, 8, L)), np.arange(L))
    z = np.take_along_axis(z, src[:, :, None, :], 3)
    plant(rng, x, z, kap)
    return pack(x, z, ts, kap, th)
def setup_inputs_corners(rng):
    x, z, ts, kap, th = parts(rng)
    for r in range(N):
        for g in range(8):
            y = (g + r) & 7
            if y == 0 and r & 1:
                x[r, g], z[r, g] = far(rng); X, Z = x[r, g], z[r, g]; s, e = first(X, Z, kap[r, g])
                v = np.abs(Z - X[:, back(X, ts[r, g], s)])[:, r * B:r * B + B]; e2 = first(X, v, kap[r, g], L)[1]
                th[r, g] = max(0, min(int(e2[int(rng.integers(0, B))]) - L, int(np.min(e)) - 1))
            elif y < 2:
                x[r, g, 0] &= 62; z[r, g, 0] |= 1; th[r, g] = 0
                if y == 1:
                    l = (0, L - 1)[int(rng.integers(0, 2))]; h = spots(mix(z[r, g]), kap[r, g], np.zeros((), np.int64))
                    x[r, g][:, h[int(rng.integers(0, 16)), l]] = z[r, g][:, l]
            elif y == 2: x[r, g], z[r, g], ts[r, g] = apart(rng, kap[r, g]); th[r, g] = 1008
            elif y == 3 and r & 1:
                x[r, g], z[r, g] = far(rng); c = np.bincount(first(x[r, g], z[r, g], kap[r, g])[1], minlength=1010)
                o = np.arange(513 + (r & 2), 1008, 4); th[r, g] = o[int(np.argmax(np.minimum(c[o], c[o + 1])))]
            elif y == 3: th[r, g] = np.sort(first(x[r, g], z[r, g], kap[r, g])[1])[L // 2]
            elif y < 6:
                us = rng.permutation(np.unique(first(x[r, g], z[r, g], kap[r, g])[0])); rest = rng.permutation(np.setdiff1d(np.arange(V), us))
                ts[r, g] = np.concatenate([us, rest] if y == 4 else [rest, us]); th[r, g] = 1008 if y == 4 else 600
            elif y == 6:
                x[r, g, 0] = 0; t = 15 * rng.integers(0, 2, V); x[r, g, 0] = ((t - mix(x[r, g])) & 15) + 16 * rng.integers(0, 4, V)
            else:
                pat = rng.integers(0, 64, (16, 3)); x[r, g] = pat[:, rng.integers(0, 3, V)]; z[r, g] = 63 * rng.integers(0, 2, (1, L)); z[r, g][:, L - 1] = 0; z[r, g][:, 0] = 63
    return pack(x, z, ts, kap, th)
def setup_inputs_crowd(rng):
    x, z, ts, kap, th = parts(rng); zero = np.zeros((), np.int64)
    for r in range(N):
        for g in range(8):
            X, Z = x[r, g], z[r, g]
            if g < 3:
                b = rng.integers(0, 16, 16); v = np.repeat(b[:, None], L, axis=1)
                for i, j in ((0, 13), (1, 12), (2, 11), (3, 10), (4, 9), (5, 8), (6, 7)):
                    fl = rng.random(L) < 0.5; v[i] = np.where(fl, b[j], b[i]); v[j] = np.where(fl, b[i], b[j])
                h = spots(mix(v), kap[r, g], zero)[:, 0]; X[:, h] = rng.integers(40, 64, (16, 16))
                X[:, h[int(rng.integers(0, 16))]] = np.clip(b + rng.integers(-2, 3, 16), 0, 63)
                odd = Z[:, 0].copy(); Z[:] = v; th[r, g] = (1008, 700, 350)[(g + r) % 3]
                if g == 1: Z[:, L - 1] = odd
                if g == 2: Z[:, 0] = odd
            elif g < 5:
                b = rng.integers(16, 44, 16); zi = b[:, None] + rng.integers(-2, 3, (16, 8)); hs = spots(mix(zi), kap[r, g], zero)[int(rng.integers(0, 16))]
                v = zi + rng.integers(-3, 4, (16, 8)); v[0] = v[0] + ((15 - mix(v)) & 15); X[:, hs] = v
                us = rng.permutation(np.unique(hs)); rest = rng.permutation(np.setdiff1d(np.arange(V), us)); a = rest[0]; X[:, a] = b
                at = 2 * np.arange(1, len(us) + 1); free = np.ones(V, bool); free[at] = False; free[0] = False
                ts[r, g, 0] = a; ts[r, g, at] = us; ts[r, g, free] = rest[1:]
                odd = Z[:, 0].copy(); Z[:] = zi[:, np.arange(L) & 7]; th[r, g] = (1008, 200)[(g + r) & 1]
                if g == 4: Z[:, 0] = odd
            elif g < 7:
                X[0] &= 62; Z[0] |= 1; th[r, g] = 0; odd = Z[:, L - 1].copy(); Z[:] = Z[:, :1].copy()
                if g == 6:
                    Z[:, L - 1] = odd; X[:, spots(mix(Z), kap[r, g], zero)[int(rng.integers(0, 16)), L - 1]] = odd
            else: Z[:] = Z[:, rng.integers(0, 4, L)].copy(); th[r, g] = 500
    return pack(x, z, ts, kap, th)
def setup_inputs_ends(rng):
    x, z, ts, kap, th = parts(rng); sh = np.array([1.0, 0.0, 0.5, 0.5, 0.9, 0.1, 0.5, 0.5]).reshape(1, 8, 1, 1)
    x = 63 * np.where(rng.random((N, 8, 1, V)) < sh, rng.integers(0, 2, (N, 8, 1, V)), rng.integers(0, 2, (N, 8, 16, V)))
    z = 63 * np.where(rng.random((N, 8, 1, L)) < sh, rng.integers(0, 2, (N, 8, 1, L)), rng.integers(0, 2, (N, 8, 16, L)))
    z[..., 0] = 63; z[..., 1] = 0; z[..., L - 2] = 0; z[..., L - 1] = 63
    kap = KM * rng.integers(0, 2, (N, 8, 16)); kap[..., 13] = 0; kap[..., 14] = KM; kap[..., 15] = 3841
    th = 1008 * rng.integers(0, 2, (N, 8)); th[:, 6] = 0; th[:, 7] = 1008
    c = (4095 * 4095 >> 5) & (V - 1); cs = np.array([c, (c + KM * 4095) & (V - 1), V - 1])
    for r in range(N):
        for g in range(8):
            y = (g + r) & 3; X = x[r, g]; X[:, cs] = (0, 63, 0, 0)[y]
            if y == 1: kap[r, g, 0] = 3841
            if y == 0: ts[r, g] = np.arange(V); X[:, V - 1] = 63
            elif y == 2: ts[r, g] = np.arange(V)[::-1]; X[:, 0] = 63
            else:
                i = int(np.flatnonzero(ts[r, g] == V - 1)[0]); j = V - 1 if y == 1 else 0; t = int(ts[r, g, j]); ts[r, g, j] = V - 1; ts[r, g, i] = t; X[:, V - 1] = 63
            if y < 2: X[:, ts[r, g, V - 2 - 16 * np.arange(K)]] = 63 * y
    X = x[N - 1, 1]; X[:] = np.where(rng.random((1, V)) < 0.1, 63 * rng.integers(0, 2, (16, V)), 0); X[0] = 0; X[:, cs] = 0
    z[N - 1, 1, 0] = 63; th[N - 1, 1] = 0
    return pack(x, z, ts, kap, th)
def setup_inputs_spread(rng):
    x, z, ts, kap, th = parts(rng)
    def odd(n):
        v = np.minimum((np.exp2(6 * rng.random((N, 8, 1, n))) * rng.random((N, 8, 16, n))).astype(np.int64), 63)
        return np.where(rng.random((N, 8, 1, n)) < 0.4, 63 - v, v)
    kap = np.minimum(np.exp2(12 * rng.random((N, 8, 16))).astype(np.int64) - 1, KM); th = np.minimum(np.exp2(10 * rng.random((N, 8))).astype(np.int64) - 1, 1008)
    return pack(odd(V), odd(L), ts, kap, th)
def setup_inputs_ties(rng):
    x, z, ts, kap, th = parts(rng); pat = rng.integers(0, 64, (N, 8, 16, 8))
    x = np.take_along_axis(pat, rng.integers(0, 8, (N, 8, 1, V)), 3); z = np.take_along_axis(pat, rng.integers(0, 8, (N, 8, 1, L)), 3)
    z = np.clip(z + rng.integers(-1, 2, z.shape) * (rng.random((N, 8, 1, L)) < 0.5), 0, 63); th = rng.integers(0, 40, (N, 8)); th[:, 3] = 0
    for r in range(N):
        for g in range(6):
            o = np.arange(V); ts[r, g] = o if g < 2 else o[::-1] if g < 4 else np.roll(o, int(rng.integers(1, V)))
    return pack(x, z, ts, kap, th)
def check_inputs(d):
    bad = []
    for k, lo, hi in (("xr", 0, 63), ("ts", 0, V - 1), ("zq", 0, 63), ("kap", 0, KM), ("th", 0, 1008)):
        a = np.asarray(d[k]).astype(np.float64)
        if not (np.min(a) >= lo and np.max(a) <= hi): bad.append("range of " + k)
        if np.any(a != np.floor(a)): bad.append("whole numbers of " + k)
    if np.any(np.sort(np.asarray(d["ts"]), axis=-1) != np.arange(V)): bad.append("permutation of ts")
    return bad
def reference(xr, ts, zq, kap, th):
    pick = np.take_along_axis
    X = xr.astype(np.float32).astype(np.int32).reshape(N, 8, 16, V); z = zq.astype(np.float32).astype(np.int32).reshape(N, 8, 16, L)
    T = ts.astype(np.int64); ka = kap.astype(np.int64).reshape(N, 8, 16); lim = th.astype(np.int64).reshape(N, 8); A = np.zeros((N, 8), np.int64)
    for rnd in range(RO):
        h = spots(mix(z), ka, A)
        xh = pick(X, h.reshape(N, 8, 1, 16 * L), 3).reshape(N, 8, 16, 16, L)
        e = np.add.reduce(np.abs(xh - z[:, :, :, None, :]), axis=2); m = np.argmin(e, axis=2)[:, :, None]
        s = pick(h, m, 2)[:, :, 0]; es = pick(e, m, 2)[:, :, 0]; xs = pick(X, s[:, :, None, :], 3)
        p = pick(np.argsort(T, axis=-1), s, 2); d = 1 + (mix(xs) & 15)
        at = np.maximum(p[:, :, None, :] - 1 - d[:, :, None, :] * np.arange(K)[:, None], 0)
        node = pick(T, at.reshape(N, 8, K * L), 2)
        xm = pick(X, node[:, :, None, :], 3).reshape(N, 8, 16, K, L)
        e = np.add.reduce(np.abs(xm - xs[:, :, :, None, :]), axis=2); k = np.argmin(e, axis=2)[:, :, None]
        n = pick(node.reshape(N, 8, K, L), k, 2)[:, :, 0]; xn = pick(X, n[:, :, None, :], 3)
        hit = es <= (lim + A)[:, :, None]
        vn = np.clip(xn + np.clip(z - xs, -2, 2), 0, 63); vs = (xs + z) >> 1
        z = np.where(hit[:, :, None, :], (z + xn) >> 1, np.abs(z - xn))
        for r in range(N):
            for g in range(8):
                lanes = np.flatnonzero(hit[r, g])
                un, i = np.unique(n[r, g, lanes], return_index=True); X[r, g][:, un] = vn[r, g][:, lanes[i]]
                us, i = np.unique(s[r, g, lanes], return_index=True); X[r, g][:, us] = vs[r, g][:, lanes[i]]
                gone = np.zeros(V, bool); gone[us] = True; old = T[r, g]
                T[r, g] = np.concatenate([old[~gone[old]], s[r, g, np.sort(lanes[i])]])
        A = L - np.add.reduce(hit.astype(np.int64), axis=2)
        z = np.ascontiguousarray(z.reshape(N, 8, 16, N, B).transpose(3, 1, 2, 0, 4)).reshape(N, 8, 16, L)
    return {"yx": X.reshape(N, 128, V).astype(np.float32).astype(BF), "yt": T.astype(np.float32), "yz": z.reshape(N, 128, L).astype(np.float32).astype(BF)}

@@ -1,0 +1,793 @@
+from concourse.bass import DstId, RemoteDMATransfer
+from concourse.mybir import AluOpType as ALU, AxisListType as AX, ActivationFunctionType as AF
+
+N, V, L, RO = 8, 2048, 256, 3
+CK = 510 * 32768
+MAGIC = float(1 << 23)
+UNITS = {(0, 0): "CCCCCCCCCCCCCCBB", (0, 1): "CCCCBBBBCCCBBBBB",
+         (1, 0): "CCCCCCBBCCCCCBBB", (1, 1): "CCCCBBBBCCCBBBBB",
+         (2, 0): "CCCCCCBBCCCCCBBB", (2, 1): "CCCCCBBBCCCCBBBB"}
+OPT = {"td": ["ssss", "ssss", "ssss"], "xt": ["vvvv", "svsv", "svsv"], "vn": "sss", "tz": "sss", "xe": "yy", "passes": 2, "wait": [0.0], "link": "s",
+       "tf_s": [(8, 16)], "tg_s": [[(8, 16)], [(0, 8), (8, 16)]], "cut1": [(0, 8), (8, 16)],
+       "cut2": [(0, 8), (8, 16)], "sum": [(0, 8), (8, 12), (12, 16)]}
+BOOST = {}
+UNITS.update({(0, 0): 'CCCCCCCCCCCCCAAC', (0, 1): 'AACCCCAAAACCCAAA', (1, 0): 'AACCCCAACCAABBAA', (1, 1): 'BBCCAACCAAAACCCC', (2, 0): 'AACCAAAAAAAACCAA', (2, 1): 'BBCCCCCCCAAAAAAA'})
+OPT.update({'td': ['ssss', 'ssss', 'ssvs'], 'xt': ['ssss', 'ssss', 'vssv'], 'vn': 'vSs', 'tz': 'svs', 'link': 'v', 'tf_s': [(8, 16)], 'tg_s': [[], []], 'xe': 'nn', 'passes': 1})
+BOOST.update({'d0': -1000, 'x0': 2000, 'o0': 3500, 'd1': 5000, 'o1': -4500, 'd2': -1000, 'x2': 23500, 'o2': 4500, 't2': 19000, 'z2': 6500, 'r1': -14500, 'p0': 500, 'r2': -18000, 'h0': -11000, 'n1': 12000, 'h2': 11500, 'e0': -8000, 's0': -1000, 'n0': -7000, 'p1': -18500, 'b': -4500, 'z0': -3000, 'm1': -2500, 't1': -2500, 'm2': -6500, 'e2': -3000, 'z1': -7000, 'e1': 8000, 't0': -6000, 'c': -14000, 'r0': -3500, 'n2': -4000, 'x1': -3500, 'h1': 15500, 's2': -5000, 's1': -1500, 'm0': 7000, 'p2': -10500, 'a': 9000})
+COST = {"cyc": 1.0, "gat": 1.56, "sca": 3.8, "pe": 0.5, "hop": 90.0, "self": 50.0, "dma": 2000.0, "rem": 5000.0}
+ESZ = {"b": 2, "f": 4, "i": 4, "u": 2}
+
+
+def plan():
+    ops, phase = [], ["a"]
+    top = {"b": 0, "f": 0, "i": 0, "u": 0}
+
+    def new(pool, n):
+        al = 64 // ESZ[pool]
+        lo = top[pool]
+        top[pool] = lo + (n + al - 1) // al * al
+        return (pool, lo, lo + n, 1, None, lo)
+
+    def sl(a, lo, hi, step=1, part=None):
+        return (a[0], a[1] + lo, a[1] + hi, step, part, a[5])
+
+    def bank(k, lo, hi):
+        return ("P%d" % k, lo, hi, 1, None, 0)
+
+    def ind(w, o):
+        return ("ind", w, o)
+
+    def cnt(a):
+        if a[0] == "ind":
+            return 16 * cnt(a[2])
+        return (a[2] - a[1] + a[3] - 1) // a[3]
+
+    def isap(a):
+        return isinstance(a, tuple)
+
+    def two(a):
+        return a[0] in ("b", "u")
+
+    def rec(eng, meth, args, outs, ins, cost):
+        rd, wr = [], []
+        for a in ins:
+            if isap(a):
+                rd.extend([a[1], a[2]] if a[0] == "ind" else [a])
+        for a in outs:
+            if a[0] == "ind":
+                wr.append(a[1])
+                rd.append(a[2])
+            else:
+                wr.append(a)
+        ops.append({"e": eng, "m": meth, "a": args, "r": rd, "w": wr, "c": cost, "p": BOOST.get(phase[0], 0.0)})
+
+    def vcost(out, a, rate):
+        n = cnt(out)
+        if out[0] == "ind":
+            return 50 + n * COST["sca"] * COST["cyc"]
+        if a is not None and a[0] == "ind":
+            return 50 + n * COST["gat"] * COST["cyc"]
+        return max(64, n * rate) * COST["cyc"]
+
+    def cp(out, a):
+        rec("v", "cp", (out, a), [out], [a], vcost(out, a, 0.5 if two(out) and two(a) else 1))
+
+    def tt(out, a, b, op):
+        rec("v", "tt", (out, a, b, op), [out], [a, b], vcost(out, a, 1 if "P" in (a[0][0], b[0][0]) else 2))
+
+    def ts(out, a, s1, op0, s2=None, op1=None):
+        rec("v", "ts", (out, a, s1, s2, op0, op1), [out], [a, s1, s2], vcost(out, a, 0.5 if two(out) and two(a) else 1))
+
+    def ms(out, c):
+        rec("v", "ms", (out, c), [out], [], vcost(out, None, 0.5 if two(out) else 1))
+
+    def red(out, a, op):
+        rec("v", "red", (out, a, op), [out], [a], vcost(a, None, 1))
+
+    def scan(out, d0, d1, init, op0, op1):
+        rec("v", "scan", (out, d0, d1, init, op0, op1), [out], [d0, d1, init],
+            vcost(out, None, 0.5 if two(out) and two(d0) and two(d1) else 1))
+
+    def act(out, a, f, scale=1.0, bias=0.0, acc=None):
+        c = 65 + cnt(out) * COST["gat"] * COST["cyc"] if a[0] == "ind" else max(64, cnt(out)) * COST["cyc"]
+        rec("s", "act", (out, a, f, scale, bias, acc), [out] + ([acc] if acc else []), [a, scale, bias], c + (20 if acc else 0))
+
+    def mm(out, l, r, start, stop):
+        rec("t", "mm", (out, l, r, start, stop), [out], [l, r], max(64, cnt(out)) * COST["pe"] * (4 if l[0] == "f" else 1))
+
+    def iota(out, pat, base=0, cm=0):
+        rec("g", "iota", (out, pat, base, cm), [out], [], 130 + 2 * cnt(out) * COST["cyc"])
+
+    def dma(q, out, a, nbytes):
+        rec(q, "dma", (out, a), [] if out[0] == "hbm" else [out], [] if a[0] == "hbm" else [a], COST["dma"] + nbytes / 250.0)
+
+    def hbm(name, idx=None):
+        return ("hbm", name, idx)
+
+    def gat(eng, out, win, off):
+        if eng == "v":
+            cp(out, ind(win, off))
+        else:
+            act(out, ind(win, off), AF.Copy)
+
+    def zr(z, r):
+        return sl(z, 15 - r, 143 - r)
+
+    def wrap(out, z, row, n, start=True):
+        for r in range(16):
+            mm(out, zr(z, r), sl(row, r, n, 16), start and r == 0, r == 15)
+
+    add, sub, mul, mx, mn = ALU.add, ALU.subtract, ALU.mult, ALU.max, ALU.min
+    band, shr = ALU.bitwise_and, ALU.arith_shift_right
+    K0, K1, D0, D1, W, R, Q, U = range(8)
+
+    Z = [new("b", L) for _ in range(RO + 1)]
+    X = new("b", V + L)
+    krow = new("i", 136)
+    tsi, tsb = new("i", 128), new("i", 128)
+    dma("y", Z[0], hbm("zq"), 65536)
+    dma("y", sl(krow, 0, 128, 1, slice(0, 1)), hbm("kap"), 512)
+    dma("y", sl(krow, 128, 136, 1, slice(0, 1)), hbm("th"), 32)
+    dma("y", sl(X, 0, V), hbm("xr"), 524288)
+    for b in range(4):
+        for gm in range(2):
+            dma("s", sl(tsi, 32 * b + 16 * gm, 32 * b + 16 * gm + 16),
+                hbm("ts", (slice(gm, 8, 2), slice(512 * b, 512 * b + 512))), 8192)
+    dma("y", tsb, hbm("ts"), 65536)
+
+    DIG = new("b", 2560)
+    ms(sl(DIG, 0, 320), 0.0)
+    for k in (320, 640, 1280):
+        act(sl(DIG, k, 2 * k), sl(DIG, 0, k), AF.Copy)
+    pI, jrow, grow, wrow = new("i", 1), new("b", 143), new("b", 128), new("f", 16)
+    iota(pI, [[0, 1]], 0, 1)
+    iota(jrow, [[1, 143]])
+    iota(sl(wrow, 0, 16, 2), [[1, 8]], 1)
+    iota(sl(wrow, 1, 15, 2), [[-1, 7]], 7)
+    iota(sl(wrow, 15, 16), [[0, 1]], 1)
+    kb = new("i", 136)
+    rec("g", "pb", (kb, sl(krow, 0, 136, 1, slice(0, 1))), [kb], [krow], 140 + 4 * 136)
+    ai, mrow, negk, lw0 = new("i", 160), new("b", L), new("f", L), new("f", 16)
+    iota(ai, [[1, 160]], 0, 160)
+    iota(grow, [[16, 8], [0, 16]])
+    iota(mrow, [[1, 16], [0, 16]])
+    iota(negk, [[-1, 16], [0, 16]])
+    iota(lw0, [[16, 16]], V, 1)
+    g16i, g16, pF, rcol, g15, g160, wcol, gth = [new(p, 1) for p in "ifffffff"]
+    ts(g16i, pI, 112, band)
+    cp(g16, g16i)
+    cp(pF, pI)
+    tt(rcol, pF, g16, sub)
+    ts(g15, g16, 15.0, add)
+    ts(g160, g16, 160.0, mul)
+    ts(gth, g16, 1.0 / 16, mul, 128.0, add)
+    m16, t16 = new("f", 16), new("f", 16)
+    ts(m16, sl(jrow, 0, 16), rcol, ALU.is_equal)
+    tt(t16, m16, wrow, mul)
+    red(wcol, t16, add)
+    ZW, ZS, ZS2, ZSN, Z1 = [new("b", 143) for _ in range(5)]
+    ts(ZW, jrow, g15, ALU.is_equal, wcol, mul)
+    ts(ZS, jrow, g15, ALU.is_equal, 32768.0, mul)
+    act(ZS2, ZS, AF.Copy, 2.0)
+    act(ZSN, ZS, AF.Copy, -1.0)
+    ts(Z1, jrow, g15, ALU.is_equal, sl(m16, 0, 1), mul)
+    I1, NI, IH, INH, INQ, I2K, I16, BO, BW, DW, IX, INE, ICK, I15 = [new("b", 128) for _ in range(14)]
+    I32 = new("f", 128)
+    crow = sl(jrow, 0, 128)
+    ts(I1, crow, pF, ALU.is_equal)
+    for t, s in ((NI, -1.0), (I2K, 2048.0), (I32, 1.0), (IH, 0.5), (INH, -0.5), (I15, 1.5), (I16, 16.0),
+                 (IX, 32.0), (INE, -0.125), (ICK, float(-CK))):
+        act(t, I1, AF.Copy, s)
+    ts(BO, grow, g16, ALU.is_equal)
+    ts(BW, grow, g16, ALU.is_equal, wcol, mul)
+    cidx, kidx = new("u", 16), new("u", 18)
+    ts(cidx, sl(jrow, 0, 16), 0.0, mul, rcol, add)
+    ts(sl(kidx, 0, 16), sl(jrow, 0, 16), g16, add)
+    ts(sl(kidx, 16, 18), sl(jrow, 0, 2), 0.0, mul, gth, add)
+    kg = new("f", 288)
+    kaprow, thc = sl(kg, 0, L), sl(kg, L, L + 1)
+    cp(kg, ind(kb, kidx))
+    LW2, LD = new("f", 32), new("f", 16)
+    LW = sl(LW2, 0, 16)
+    ts(LW, lw0, g16, sub)
+    ts(sl(LW2, 16, 32), lw0, g16, sub)
+    ts(LD, LW, 256.0, add)
+    ones = new("b", L)
+    ms(ones, 1.0)
+    half, thr, big0, big, pw16, pcol = new("f", L), new("b", L), new("f", 1), new("f", 1), new("f", 16), new("f", 1)
+    ms(half, 0.5)
+    ms(sl(half, 0, L, 16), 1.0)
+    ms(big0, 2.0 ** 60)
+    ts(big, big0, 2.0 ** 61, mul)
+    scan(thr, half, negk, big, mul, mx)
+    tt(pw16, sl(thr, 0, 16), m16, mul)
+    red(big0, pw16, add)
+    ts(pcol, big0, 2.0 ** -50, mul, 2.0 ** -50, mul)
+    ts(DW, grow, g16, ALU.is_equal, pcol, mul)
+
+    def digits(src, n, table, q):
+        loi, hii, lo, hi = new("i", n), new("i", n), new("b", n), new("b", n)
+        ts(loi, src, 15, band)
+        ts(hii, src, 4, shr)
+        cp(lo, loi)
+        ts(hi, hii, 2.0, mul)
+        dma(q, sl(table, 0, 16 * n, 1, slice(0, 128, 16)), lo, 256 * n)
+        dma(q, sl(table, 0, 16 * n, 1, slice(14, 128, 16)), hi, 256 * n)
+
+    ab = new("i", 160)
+    ts(ab, ai, g160, sub)
+    digits(ab, 160, DIG, "y")
+    TD = [new("b", V + L) for _ in range(RO)] + [new("b", V)]
+    iota(sl(TD[0], 0, V), [[0, V]])
+    digits(tsb, 128, TD[0], "y")
+    G = [new("b", 2560) for _ in range(RO)]
+    M = [new("b", 2560) for _ in range(RO)]
+    CU = [new("b", 2560) for _ in range(RO)]
+    for t in range(RO):
+        for tb, n in ((G[t], 2560 if t == 0 else 2320), (M[t], V)):
+            for k in range(0, n, 640):
+                iota(sl(tb, k, min(n, k + 640)), [[0, min(n, k + 640) - k]])
+    tsf, tst, tsw = new("f", 128), new("f", 128), new("u", 128)
+    cp(tsf, tsi)
+    rec("v", "tr", (tst, tsf), [tst], [tsf], 128 * COST["cyc"])
+    cp(tsw, tst)
+    PD = new("b", V + L)
+    phase[0] = "b"
+    for k in range(8):
+        cp(ind(sl(PD, 0, V), sl(tsw, 16 * k, 16 * k + 16)), sl(DIG, 256 * k, 256 * k + 256))
+    XT = [new("b", 2560), new("b", 2560)]
+
+    def regather(out, win, off, engs):
+        n = 128 // len(engs)
+        for k, e in enumerate(engs):
+            gat(e, sl(out, 16 * n * k, 16 * n * (k + 1)), win, sl(off, n * k, n * (k + 1)))
+
+    phase[0] = "c"
+    regather(XT[0], sl(X, 0, V), tsw, OPT["xt"][0])
+    colA, thA, thK = new("f", 1), new("f", 1), new("f", 1)
+    ms(colA, -13.0)
+    thB, thL = new("f", 1), new("f", 1)
+    ts(thA, thc, 0.5, add)
+    ts(thK, thc, -509.0, add, 32768.0, mul)
+    ts(thB, thc, 128.5, add)
+    ts(thL, thc, 128.0 - 509.0, add, 32768.0, mul)
+
+    DT, AB = new("b", 16 * L), new("b", 16 * L)
+    SH = new("b", V)
+    EQ = [new("b", 2176), new("b", 2176)]
+    dbank = [0]
+
+    def nearest(units, win, off, zrow, h32, centre):
+        for lo, hi in OPT["sum"]:
+            m = lo
+            while m < hi:
+                e = m
+                while e < hi and units[e] == units[m] and e - m < 2:
+                    e += 1
+                d, a = sl(DT, L * m, L * e), sl(AB, L * m, L * e)
+                if units[m] == "C":
+                    gat("s", d, win, sl(off, 16 * m, 16 * e))
+                    bk = (D0, D1)[dbank[0] & 1]
+                    dbank[0] += 1
+                    for j in range(m, e):
+                        o = bank(bk, L * (j - m), L * (j - m + 1))
+                        mm(o, I1, sl(DT, L * j, L * j + L), True, False)
+                        mm(o, NI, zrow, False, True)
+                    act(a, bank(bk, 0, L * (e - m)), AF.Abs)
+                else:
+                    for j in range(m, e):
+                        tt(sl(DT, L * j, L * j + L), ind(win, sl(off, 16 * j, 16 * j + 16)), zrow, sub)
+                    if units[m] == "A":
+                        act(a, d, AF.Abs)
+                    else:
+                        ts(a, d, 0.0, mx)
+                m = e
+            bk, base = (K0, 0) if lo < 8 else (K1, 8)
+            whole = bank(bk, 16 * (lo - base), 16 * (hi - base))
+            mm(whole, I2K, sl(mrow, 16 * lo, 16 * hi), True, False)
+            if centre:
+                mm(whole, ICK, sl(ones, 16 * lo, 16 * hi), False, False)
+            last = "B" in units[lo:hi]
+            if not last:
+                mm(whole, I32, sl(h32, 16 * lo, 16 * hi), False, False)
+            m = lo
+            while m < hi:
+                e = m
+                while e < hi and (units[e] == "B") == (units[m] == "B"):
+                    e += 1
+                o = bank(bk, 16 * (m - base), 16 * (e - base))
+                for r in range(16):
+                    if units[m] == "B":
+                        mm(o, zr(ZSN, r), sl(DT, L * m + r, L * e, 16), False, False)
+                for r in range(16):
+                    mm(o, zr(ZS2 if units[m] == "B" else ZS, r), sl(AB, L * m + r, L * e, 16), False, e == hi and r == 15 and not last)
+                m = e
+            if last:
+                mm(whole, I32, sl(h32, 16 * lo, 16 * hi), False, True)
+        k0, k1, k2, k3, key = new("f", 128), new("f", 128), new("f", 64), new("f", 32), new("i", 16)
+        act(k0, bank(K0, 0, 128), AF.Copy)
+        tt(k1, bank(K1, 0, 128), k0, mn)
+        tt(k2, sl(k1, 0, 64), sl(k1, 64, 128), mn)
+        tt(k3, sl(k2, 0, 32), sl(k2, 32, 64), mn)
+        tt(key, sl(k3, 0, 16), sl(k3, 16, 32), mn)
+        vi, vu = new("i", 16), new("u", 16)
+        ts(vi, key, V - 1, band)
+        cp(vu, vi)
+        return key, vi, vu
+
+    def firsts(dig, kw, miss, eq, bk):
+        kr, km, fr, fw = new("u", L), new("f", 16), new("b", L), new("f", 16)
+        mm(bank(Q, 256, 512), BW, dig, True, True)
+        cp(kr, bank(Q, 256, 512))
+        tt(km, kw, miss, add)
+        mm(bank(Q, 0, L), NI, thr, True, False)
+        o = 0
+        for c in range(16):
+            n = L - 16 * c
+            ts(sl(eq, o, o + n), sl(kr, 16 * c, L), sl(km, c, c + 1), ALU.is_equal, 2.0 ** (99 - 15 * c), mul)
+            mm(bank(Q, 16 * c, L), DW, sl(eq, o, o + n), False, c == 15)
+            o += n
+        act(fr, bank(Q, 0, L), AF.Sign)
+        wrap(bank(bk, 0, 16), Z1, fr, L)
+        ts(fw, bank(bk, 0, 16), 0.0, ALU.is_lt)
+        return fw
+
+    ci, hi_, tf, h32 = new("i", L), new("i", L), new("f", L), new("f", L)
+    atf, a32, tg = new("f", L), new("f", L), new("f", L)
+    for t in range(RO):
+        z, xt = Z[t], sl(XT[t & 1], 0, V)
+        phase[0] = "h%d" % t
+        u2, sq, a2, hu = new("f", 16), new("f", 16), new("i", 16), new("u", L)
+        wrap(bank(W, 0, 16), ZW, z, L)
+        cp(u2, bank(W, 0, 16))
+        tt(sq, bank(W, 0, 16), u2, mul)
+        ts(a2, sq, colA, add, 1.0 / 32, mul)
+        for lo, hi in OPT["cut1"]:
+            a, b = 16 * lo, 16 * hi
+            if (lo, hi) in OPT["tf_s"]:
+                for m in range(lo, hi):
+                    act(sl(tf, 16 * m, 16 * m + 16), u2, AF.Copy, sl(kaprow, 16 * m, 16 * m + 1))
+            else:
+                tt(sl(tf, a, b), ind(u2, sl(cidx, lo, hi)), sl(kaprow, a, b), mul)
+            tt(sl(ci, a, b), ind(a2, sl(cidx, lo, hi)), sl(tf, a, b), add)
+            ts(sl(hi_, a, b), sl(ci, a, b), V - 1, band)
+            cp(sl(hu, a, b), sl(hi_, a, b))
+            ts(sl(h32, a, b), sl(hi_, a, b), float(-CK), add)
+        phase[0] = "s%d" % t
+        key, si, su = nearest(UNITS[(t, 0)], sl(X, 0, V), hu, z, h32, False)
+        phase[0] = "m%d" % t
+        xp = new("b", 2 * L)
+        xs, pd = sl(xp, 0, L), sl(xp, L, 2 * L)
+        gat("v", xs, sl(X, 0, V), su)
+        gat("s", pd, sl(PD, 0, V), su)
+        wrap(bank(W, 0, 32), ZW, xp, 2 * L)
+        i2, dm, d2, au = new("i", 32), new("i", 16), new("f", 16), new("u", L)
+        cp(i2, bank(W, 0, 32))
+        tau = p = sl(i2, 16, 32)
+        for k in range(t):
+            pu, cg, p2 = new("u", 16), new("b", L), new("f", 16)
+            cp(pu, p)
+            gat(OPT["link"], cg, sl(CU[k], 0, 2560 if k == 0 else 2320), pu)
+            wrap(bank(W, 0, 16), Z1, cg, L)
+            tt(p2, p, bank(W, 0, 16), sub)
+            p = p2
+        ts(dm, sl(i2, 0, 16), 15, band)
+        ts(d2, dm, 1.0, add)
+        for lo, hi in OPT["cut2"]:
+            a, b = 16 * lo, 16 * hi
+            if (lo, hi) in OPT["tg_s"][min(t, 1)]:
+                for m in range(lo, hi):
+                    act(sl(tg, 16 * m, 16 * m + 16), d2, AF.Copy, float(-m))
+            else:
+                tt(sl(tg, a, b), ind(d2, sl(cidx, lo, hi)), sl(negk, a, b), mul)
+            tt(sl(atf, a, b), ind(p, sl(cidx, lo, hi)), sl(tg, a, b), add)
+            ts(sl(au, a, b), sl(atf, a, b), -1.0, add)
+            act(sl(a32, a, b), sl(atf, a, b), AF.Relu, 1.0, -1.0)
+        phase[0] = "p%d" % t
+        hitw, miss = new("f", 16), new("f", 16)
+        ts(hitw, key, thK, ALU.is_lt)
+        ts(miss, key, thK, ALU.is_ge, 4096.0, mul)
+        adz, sgn, sg, zh, cc, vs, dz, v0 = [new("b", L) for _ in range(8)]
+        mm(bank(U, 0, L), I1, z, True, False)
+        mm(bank(U, 0, L), NI, xs, False, True)
+        act(adz, bank(U, 0, L), AF.Abs)
+        act(dz, bank(U, 0, L), AF.Copy)
+        ts(cc, dz, -2.0, mx, 2.0, mn)
+        mm(bank(U, L, 2 * L), BO, adz, True, True)
+        nsum = new("f", 1)
+        act(sgn, bank(U, L, 2 * L), AF.Sign, -1.0, thA, nsum)
+        mm(bank(U, 0, L), I1, z, True, False)
+        mm(bank(U, 0, L), IX, sgn, False, True)
+        act(zh, bank(U, 0, L), AF.Relu, 1.0, -32.0)
+        mm(bank(U, 0, L), IH, z, True, False)
+        mm(bank(U, 0, L), IH, xs, False, True)
+        act(v0, bank(U, 0, L), AF.Identity, 1.0, 159.75)
+        vs = sl(XT[t & 1], V, V + L)
+        ts(vs, v0, -160.0, add)
+        if t + 1 < RO:
+            colA, thA, thK = new("f", 1), new("f", 1), new("f", 1)
+            act(colA, nsum, AF.Identity, -16.0, 4083.0)
+            act(thA, nsum, AF.Identity, -0.5, thB)
+            act(thK, nsum, AF.Identity, -16384.0, thL)
+        phase[0] = "d%d" % t
+        dd, okw, t32, q32, uu = new("f", 32), new("f", 16), new("f", 32), new("f", 32), new("u", 48)
+        tt(sl(dd, 0, 16), si, LW, sub)
+        tt(sl(dd, 16, 32), p, LW, sub)
+        fs = firsts(pd, tau, miss, EQ[0], U)
+        tt(okw, fs, hitw, mul)
+        tt(sl(t32, 0, 16), sl(dd, 0, 16), okw, mul)
+        tt(sl(t32, 16, 32), sl(dd, 16, 32), okw, mul)
+        tt(q32, t32, LW2, add)
+        q, sou, qu = sl(q32, 16, 32), sl(uu, 0, 16), sl(uu, 16, 48)
+        cp(sl(uu, 0, 32), q32)
+        ts(sl(uu, 32, 48), q, 1.0, add)
+        gat("s", sl(TD[t], V, V + L), sl(DIG, 0, V), su)
+        phase[0] = "x%d" % t
+        cp(ind(X, sou), vs)
+        if t + 1 < RO:
+            cp(ind(PD, sou), sl(DIG, V + L * t, V + L * t + L))
+        phase[0] = "o%d" % t
+        gw = 2560 if t == 0 else 2320
+        cp(ind(sl(G[t], 0, V + L), sl(qu, 0, 16)), ones)
+        for k in range(0, gw, 640):
+            e = min(gw, k + 640)
+            scan(sl(CU[t], k, e), sl(G[t], k, e), sl(G[t], k, e), 0.0 if k == 0 else sl(CU[t], k - 1, k), add, mx)
+        cg, cw, fl, t1, a1, ps, pu = new("b", 2 * L), new("f", 32), new("f", 16), new("f", 16), new("f", 16), new("f", 16), new("u", 16)
+        gat("s", cg, sl(CU[t], 0, gw), qu)
+        wrap(bank(U, 0, 32), Z1, cg, 2 * L)
+        act(cw, bank(U, 0, 32), AF.Identity, 1.0, -1.0)
+        tt(fl, sl(cw, 16, 32), sl(cw, 0, 16), sub)
+        tt(a1, q, sl(cw, 16, 32), sub)
+        tt(t1, fl, LD, mul)
+        tt(ps, t1, a1, mx)
+        cp(pu, ps)
+        cp(ind(M[t], pu), sl(cg, L, 2 * L))
+        for k in range(0, V, 512):
+            scan(sl(SH, k, k + 512), sl(M[t], k, k + 512), sl(M[t], k, k + 512), 0.0 if k == 0 else sl(SH, k - 1, k), mx, mx)
+        ou = new("u", 128)
+        for k in (0, 64):
+            mm(bank(U, k, k + 64), I16, sl(jrow, k, k + 64), True, False)
+            wrap(bank(U, k, k + 64), Z1, sl(SH, 16 * k, 16 * k + 1024), 1024, False)
+            ts(sl(ou, k, k + 64), bank(U, k, k + 64), rcol, add)
+        phase[0] = "t%d" % t
+        regather(TD[t + 1], TD[t], ou, OPT["td"][t])
+        if t + 1 < RO and OPT["xe"][t] == "y":
+            pass
+        elif t + 1 < RO:
+            tw = new("u", 128)
+            for k in (0, 64):
+                wrap(bank(U, k, k + 64), ZW, sl(TD[t + 1], 16 * k, 16 * k + 1024), 1024)
+                cp(sl(tw, k, k + 64), bank(U, k, k + 64))
+        else:
+            for r in range(16):
+                mm(bank(U, 0, 128), zr(ZW, r), sl(TD[t + 1], 128 * r, 128 * r + 128), r == 0, r == 15)
+            act(tst, bank(U, 0, 128), AF.Copy)
+            dma("s", hbm("yt"), tst, 65536)
+        phase[0] = "n%d" % t
+        _, ni, nu = nearest(UNITS[(t, 1)], xt, au, xs, a32, True)
+        phase[0] = "z%d" % t
+        tz, av, zs, ng = new("b", L), new("b", L), new("b", L), new("b", 2 * L)
+        nd = sl(ng, 0, L)
+        mm(bank(R, 0, L), I1, z, True, False)
+        mm(bank(R, 0, L), INH, zh, False, False)
+        mm(bank(R, 0, L), INE, sgn, False, False)
+        vn0 = new("b", L)
+        if OPT["tz"][t] == "v":
+            act(sg, sgn, AF.Identity, 0.75, -0.25)
+            tt(tz, ind(xt, nu), sg, mul)
+            mm(bank(R, 0, L), I1, tz, False, True)
+        else:
+            gat("s", vn0, xt, nu)
+            mm(bank(W, 0, L), IX, sgn, True, False)
+            mm(bank(W, 0, L), I1, vn0, False, True)
+            act(tz, bank(W, 0, L), AF.Relu, 1.0, -32.0)
+            mm(bank(R, 0, L), NI, vn0, False, False)
+            mm(bank(R, 0, L), I15, tz, False, True)
+        act(av, bank(R, 0, L), AF.Abs, 1.0, -0.125)
+        ts(zs, av, MAGIC, add, -MAGIC, add)
+        rec("g", "send", (t, zs, Z[t + 1]), [], [zs], 600)
+        rec("s", "own", (t, zs, Z[t + 1]), [Z[t + 1]], [zs], 64)
+        rec("x", "arr", (t, len(ops) - 2), [Z[t + 1]], [], COST["rem"])
+        phase[0] = "e%d" % t
+        gat("s", nd, sl(TD[t], 0, V), nu)
+        gat("s", sl(ng, L, 2 * L), sl(G[t], 0, V), nu)
+        nw, vn, nou, hk = new("f", 32), new("b", L), new("u", 16), new("f", 16)
+        wrap(bank(W, 0, 32), ZW, ng, 2 * L)
+        act(nw, bank(W, 0, 32), AF.Copy)
+        dn, de, tn, on = [new("f", 16) for _ in range(4)]
+        tt(hk, hitw, sl(nw, 16, 32), ALU.is_gt)
+        tt(dn, sl(nw, 0, 16), LW, sub)
+        tt(de, dn, hk, mul)
+        fn = firsts(nd, sl(nw, 0, 16), miss, EQ[1], W)
+        tt(tn, de, fn, mul)
+        tt(on, tn, LW, add)
+        v1, v2 = new("b", L), new("b", L)
+        if OPT["vn"][t] == "v":
+            tt(v1, ind(xt, nu), cc, add)
+            ts(vn, v1, 0.0, mx, 63.0, mn)
+        else:
+            if OPT["tz"][t] == "v":
+                gat("s", vn0, xt, nu)
+            mm(bank(R, 0, L), I1, cc, True, False)
+            mm(bank(R, 0, L), I1, vn0, False, True)
+            act(v1, bank(R, 0, L), AF.Relu)
+            if OPT["vn"][t] == "s":
+                ts(vn, v1, 63.0, mn)
+            else:
+                act(v2, v1, AF.Relu, -1.0, 63.0)
+                act(vn, v2, AF.Identity, -1.0, 63.0)
+        cp(nou, on)
+        cp(ind(X, nou), vn)
+        if t + 1 < RO and OPT["xe"][t] == "y":
+            d3, e3, t3, o3, u3 = new("f", 16), new("f", 16), new("f", 16), new("f", 16), new("u", 16)
+            tt(d3, ni, LD, sub)
+            tt(e3, d3, hk, mul)
+            tt(t3, e3, fn, mul)
+            tt(o3, t3, LD, add)
+            cp(u3, o3)
+            cp(ind(XT[t & 1], u3), vn)
+            phase[0] = "r%d" % t
+            regather(XT[(t + 1) & 1], sl(XT[t & 1], 0, V + L), ou, OPT["xt"][t + 1])
+        elif t + 1 < RO:
+            phase[0] = "r%d" % t
+            regather(XT[(t + 1) & 1], sl(X, 0, V), tw, OPT["xt"][t + 1])
+    dma("y", hbm("yx"), sl(X, 0, V), 524288)
+    dma("s", hbm("yz"), Z[RO], 65536)
+    return ops, top
+
+
+def depend(ops):
+    hist = {}
+    deps = []
+    for i, o in enumerate(ops):
+        d = set()
+        if o["m"] == "arr":
+            d.add(o["a"][1])
+        for aps, isw in ((o["r"], False), (o["w"], True)):
+            for a in aps:
+                if a[0][0] == "P":
+                    lo, hi, w = 0, 512, True
+                else:
+                    lo, hi, w = a[1], a[2], isw
+                h = hist.setdefault((a[0], a[5]), [])
+                keep = []
+                for e in h:
+                    hitx = e[0] < hi and lo < e[1]
+                    if hitx and (w or e[2]) and e[3] != i and not (o["m"] == "arr" and ops[e[3]]["m"] == "own"):
+                        d.add(e[3])
+                    if not (w and lo <= e[0] and e[1] <= hi and o["m"] != "arr"):
+                        keep.append(e)
+                keep.append((lo, hi, w, i))
+                hist[(a[0], a[5])] = keep
+        deps.append(d)
+    return deps
+
+
+def schedule(ops, deps=None):
+    n = len(ops)
+    deps = depend(ops) if deps is None else deps
+    succ = [[] for _ in range(n)]
+    for i in range(n):
+        for j in deps[i]:
+            succ[j].append(i)
+
+    def lag(j, i):
+        if ops[j]["e"] == ops[i]["e"] and ops[j]["m"] != "dma":
+            return 0.0 if ops[i]["e"] == "t" else COST["self"]
+        return COST["hop"]
+
+    lvl = [0.0] * n
+    for i in range(n - 1, -1, -1):
+        lvl[i] = ops[i]["c"] + max([lvl[k] + lag(i, k) for k in succ[i]] + [0.0])
+    cost = [o["c"] for o in ops]
+    hold = [60.0 if o["m"] == "dma" else (0.0 if o["m"] == "arr" else o["c"]) for o in ops]
+    pre = [[(j, lag(j, i)) for j in deps[i]] for i in range(n)]
+    post = [[(k, lag(i, k)) for k in succ[i]] for i in range(n)]
+
+    def place(seq, before, back):
+        busy = {e: ([], []) for e in "vstgyx"}
+        start, end = [0.0] * n, [0.0] * n
+        for i in seq:
+            t = 0.0
+            for j, l in before[i]:
+                if end[j] + l > t:
+                    t = end[j] + l
+            off = cost[i] - hold[i] if back else 0.0
+            t += off
+            h = hold[i]
+            if h:
+                bs, be = busy[ops[i]["e"]]
+                lo, hi = 0, len(be)
+                while lo < hi:
+                    mid = (lo + hi) // 2
+                    if be[mid] <= t:
+                        lo = mid + 1
+                    else:
+                        hi = mid
+                while lo < len(bs) and t + h > bs[lo]:
+                    t = max(t, be[lo])
+                    lo += 1
+                bs.insert(lo, t)
+                be.insert(lo, t + h)
+            start[i] = t - off
+            end[i] = start[i] + cost[i]
+        return start, end
+
+    def sweep(pri, wait):
+        start, end, rdy = [0.0] * n, [0.0] * n, [0.0] * n
+        left = [len(p) for p in pre]
+        pool = {e: [] for e in "vstgyx"}
+        free = {e: 0.0 for e in "vstgyx"}
+        for i in range(n):
+            if not left[i]:
+                pool[ops[i]["e"]].append(i)
+        for _ in range(n):
+            bt, be = None, None
+            for e, p in pool.items():
+                if p:
+                    t = max(free[e], min([rdy[i] for i in p]))
+                    if bt is None or t < bt:
+                        bt, be = t, e
+            p = pool[be]
+            i = max([k for k in p if rdy[k] <= bt + wait], key=lambda k: pri[k] - (rdy[k] - bt if rdy[k] > bt else 0.0))
+            p.remove(i)
+            start[i] = max(bt, rdy[i])
+            end[i] = start[i] + cost[i]
+            free[be] = start[i] + hold[i]
+            for k, l in post[i]:
+                if end[i] + l > rdy[k]:
+                    rdy[k] = end[i] + l
+                left[k] -= 1
+                if not left[k]:
+                    pool[ops[k]["e"]].append(k)
+        return start, end
+
+    def polish(start, end):
+        s2, e2 = place(sorted(range(n), key=lambda k: (-end[k], -k)), post, True)
+        return place(sorted(range(n), key=lambda k: (-e2[k], k)), pre, False), e2
+
+    best = None
+    for wait in OPT["wait"]:
+        pri = lvl
+        for _ in range(OPT["passes"]):
+            start, end = sweep([pri[k] + ops[k]["p"] for k in range(n)], wait)
+            (s3, e3), pri = polish(start, end)
+            for s, e in ((start, end), (s3, e3)):
+                if best is None or max(e) < best[0]:
+                    best = (max(e), s, e)
+    start, end = best[1], best[2]
+    order = sorted(range(n), key=lambda k: (start[k], k))
+    return deps, order, start, end
+
+
+OPS, TOP = plan()
+DEPS, ORDER, START, END = schedule(OPS)
+NDMA = sum(1 for o in OPS if o["m"] == "dma")
+SCRATCH = {"b": ("sbuf", [128, TOP["b"]], "bfloat16"), "f": ("sbuf", [128, TOP["f"]], "float32"),
+           "i": ("sbuf", [128, TOP["i"]], "int32"), "u": ("sbuf", [128, TOP["u"]], "uint16")}
+for _k in range(8):
+    SCRATCH["P%d" % _k] = ("psum", [128, 512], "float32")
+SEMAPHORES = ["qv", "qs", "qt", "qg", "left"] + ["arr%d" % _k for _k in range(RO)] + ["d%d" % _k for _k in range(NDMA)]
+
+
+def routes(T, topo, src):
+    dsts = [c for c in T.cores if c != src]
+    dsts.sort(key=lambda c: (len(topo.engines(src, c)), (T.rank_of(c) - T.rank_of(src)) % N))
+    used, out = set(), []
+    for k, c in enumerate(dsts):
+        can = topo.engines(src, c)
+        free = [e for e in can if e not in used]
+        alike = sum(1 for x in dsts[k:] if topo.engines(src, x) == can)
+        w = 1
+        while 2 * w * alike <= len(free):
+            w *= 2
+        take = free[:w]
+        used.update(take)
+        out.append((T.rank_of(c), take))
+    return out
+
+
+def rank_program(g, core, T, topo):
+    rank = T.rank_of(core)
+    if rank is None:
+        return
+    B = L // N
+    queue = {"v": g.vector, "s": g.scalar, "t": g.tensor, "g": g, "y": g.sync}
+    mine = routes(T, topo, core)
+    expect = sum(len(e) for c in T.cores if c != core for r, e in routes(T, topo, c) if r == rank)
+
+    def ap(a):
+        if not isinstance(a, tuple):
+            return a
+        if a[0] == "ind":
+            return ap(a[1]).indirect(ap(a[2]))
+        if a[0] == "hbm":
+            return T[a[1]][:] if a[2] is None else T[a[1]][a[2]]
+        part = slice(0, 128) if a[4] is None else a[4]
+        return T[a[0]][part, a[1]:a[2]] if a[3] == 1 else T[a[0]][part, a[1]:a[2]:a[3]]
+
+    def needs(i):
+        return [j for j in DEPS[i] if not (OPS[j]["e"] == "t" and OPS[i]["e"] == "t") and OPS[i]["m"] != "arr"]
+
+    pos = {i: k for k, i in enumerate(ORDER)}
+    seen, wanted, waits = {}, set(), {}
+    for i in ORDER:
+        e, w = OPS[i]["e"], {}
+        for j in needs(i):
+            key = j if OPS[j]["m"] in ("dma", "arr") else OPS[j]["e"]
+            if pos[j] > seen.get((e, key), -1) and (key not in w or pos[j] > pos[w[key]]):
+                w[key] = j
+        for key, j in w.items():
+            seen[(e, key)] = pos[j]
+            wanted.add(j)
+        waits[i] = list(w.values())
+    mark, count, nd, left = {}, {e: 0 for e in "vstg"}, 0, 0
+    for i in ORDER:
+        o = OPS[i]
+        e, m, a = o["e"], o["m"], o["a"]
+        if m == "arr":
+            mark[i] = (T.sem["arr%d" % a[0]], expect)
+            continue
+        q = queue[e]
+        for j in waits[i]:
+            q.wait_ge(mark[j][0], mark[j][1])
+        x = [ap(y) for y in a]
+        if m == "send":
+            tr = []
+            for r, eng in mine:
+                rid, pid = topo.addr(T.cores[r], core)
+                tr.append(RemoteDMATransfer(
+                    dst_ids=[DstId(rid=rid, pnc=pid)], dma_engine_mask=sum(1 << k for k in eng),
+                    remote_sem=T.sem["arr%d" % a[0]], src=T.b[:, a[1][1] + B * r:a[1][1] + B * r + B],
+                    dst=T.b[:, a[2][1] + B * rank:a[2][1] + B * rank + B]))
+                left += len(eng)
+            g.remote_dma_fused(tr, local_sem=T.sem.left)
+            continue
+        if m == "dma":
+            q.dma_start(x[0], x[1]).then_inc(T.sem["d%d" % nd], 16)
+            mark[i] = (T.sem["d%d" % nd], 16)
+            nd += 1
+            continue
+        if m == "cp":
+            ins = q.tensor_copy(x[0], x[1])
+        elif m == "tt":
+            ins = q.tensor_tensor(x[0], x[1], x[2], x[3])
+        elif m == "ts":
+            ins = q.tensor_scalar(x[0], x[1], x[2], None, x[4]) if x[5] is None else q.tensor_scalar(*x)
+        elif m == "ms":
+            ins = q.memset(x[0], x[1])
+        elif m == "red":
+            ins = q.tensor_reduce(x[0], x[1], AX.X, x[2])
+        elif m == "scan":
+            ins = q.tensor_tensor_scan(*x)
+        elif m == "tr":
+            ins = q.transpose(x[0], x[1])
+        elif m == "act":
+            kw = {}
+            if a[3] != 1.0:
+                kw["scale"] = x[3]
+            if a[4] != 0.0:
+                kw["bias"] = x[4]
+            if a[5] is not None:
+                kw["accum_out"] = x[5]
+            ins = q.activation(x[0], x[1], x[2], **kw)
+        elif m == "own":
+            ins = q.activation(T.b[:, a[2][1] + B * rank:a[2][1] + B * rank + B],
+                               T.b[:, a[1][1] + B * rank:a[1][1] + B * rank + B], AF.Copy)
+        elif m == "mm":
+            ins = q.matmul(*x)
+        elif m == "iota":
+            if a[0][0] == "i":
+                ins = g.iota(x[0], x[1], x[2], x[3])
+            else:
+                ins = g.iota(x[0], x[1], x[2], x[3], allow_small_or_imprecise_dtypes=True)
+        else:
+            ins = g.partition_broadcast(x[0], x[1], 128)
+        if i in wanted:
+            count[e] += 1
+            ins.then_inc(T.sem["q" + e], 1)
+            mark[i] = (T.sem["q" + e], count[e])
+    for i in ORDER:
+        if OPS[i]["m"] == "dma" and i not in wanted:
+            g.wait_ge(mark[i][0], 16)
+    g.wait_ge(T.sem.left, left)

@@ -1,20 +1,18 @@
+import math
 from concourse.bass import DstId, RemoteDMATransfer
 from concourse.mybir import AluOpType as ALU, AxisListType as AX, ActivationFunctionType as AF
 
 N, V, L, RO = 8, 2048, 256, 3
 CK = 510 * 32768
-MAGIC = float(1 << 23)
-UNITS = {(0, 0): "CCCCCCCCCCCCCCBB", (0, 1): "CCCCBBBBCCCBBBBB",
-         (1, 0): "CCCCCCBBCCCCCBBB", (1, 1): "CCCCBBBBCCCBBBBB",
-         (2, 0): "CCCCCCBBCCCCCBBB", (2, 1): "CCCCCBBBCCCCBBBB"}
-OPT = {"td": ["ssss", "ssss", "ssss"], "xt": ["vvvv", "svsv", "svsv"], "vn": "sss", "tz": "sss", "xe": "yy", "passes": 2, "wait": [0.0], "link": "s",
-       "tf_s": [(8, 16)], "tg_s": [[(8, 16)], [(0, 8), (8, 16)]], "cut1": [(0, 8), (8, 16)],
-       "cut2": [(0, 8), (8, 16)], "sum": [(0, 8), (8, 12), (12, 16)]}
+OFF = 192.0
+FR = 1024.0
+UNITS = {(t, k): "CCCC BBBB CCAA AAAA" for t in range(RO) for k in range(2)}
+UNITS[(0, 0)] = "CCCC CCCC CCCC CCAA"
+OPT = {"xt": ["ssss", "ssss", "svsv"], "pd": 4, "x0": "ssvv", "tries": 4500, "seed": 2, "run": 8, "link": "sss", "xs": "vvv",
+       "vn0": "sss", "cc": "sss", "tz": "sss", "dig": "s", "mat": "v", "tf": [4, 4, 4], "at": [4, 4, 4],
+       "app": "ss", "nd": "vvv", "vn": "sss", "ek": "iis", "cut": [(0, 8), (8, 16)]}
 BOOST = {}
-UNITS.update({(0, 0): 'CCCCCCCCCCCCCAAC', (0, 1): 'AACCCCAAAACCCAAA', (1, 0): 'AACCCCAACCAABBAA', (1, 1): 'BBCCAACCAAAACCCC', (2, 0): 'AACCAAAAAAAACCAA', (2, 1): 'BBCCCCCCCAAAAAAA'})
-OPT.update({'td': ['ssss', 'ssss', 'ssvs'], 'xt': ['ssss', 'ssss', 'vssv'], 'vn': 'vSs', 'tz': 'svs', 'link': 'v', 'tf_s': [(8, 16)], 'tg_s': [[], []], 'xe': 'nn', 'passes': 1})
-BOOST.update({'d0': -1000, 'x0': 2000, 'o0': 3500, 'd1': 5000, 'o1': -4500, 'd2': -1000, 'x2': 23500, 'o2': 4500, 't2': 19000, 'z2': 6500, 'r1': -14500, 'p0': 500, 'r2': -18000, 'h0': -11000, 'n1': 12000, 'h2': 11500, 'e0': -8000, 's0': -1000, 'n0': -7000, 'p1': -18500, 'b': -4500, 'z0': -3000, 'm1': -2500, 't1': -2500, 'm2': -6500, 'e2': -3000, 'z1': -7000, 'e1': 8000, 't0': -6000, 'c': -14000, 'r0': -3500, 'n2': -4000, 'x1': -3500, 'h1': 15500, 's2': -5000, 's1': -1500, 'm0': 7000, 'p2': -10500, 'a': 9000})
-COST = {"cyc": 1.0, "gat": 1.56, "sca": 3.8, "pe": 0.5, "hop": 90.0, "self": 50.0, "dma": 2000.0, "rem": 5000.0}
+COST = {"cyc": 1.04, "gat": 1.56, "sca": 3.8, "pe": 0.5, "hop": 150.0, "self": 100.0, "dma": 2000.0, "rem": 5000.0}
 ESZ = {"b": 2, "f": 4, "i": 4, "u": 2}
 
 
@@ -59,7 +57,7 @@ def plan():
                 rd.append(a[2])
             else:
                 wr.append(a)
-        ops.append({"e": eng, "m": meth, "a": args, "r": rd, "w": wr, "c": cost, "p": BOOST.get(phase[0], 0.0)})
+        ops.append({"e": eng, "m": meth, "a": args, "r": rd, "w": wr, "c": cost, "p": BOOST.get(phase[0], 0.0), "ph": phase[0]})
 
     def vcost(out, a, rate):
         n = cnt(out)
@@ -98,11 +96,22 @@ def plan():
     def iota(out, pat, base=0, cm=0):
         rec("g", "iota", (out, pat, base, cm), [out], [], 130 + 2 * cnt(out) * COST["cyc"])
 
-    def dma(q, out, a, nbytes):
-        rec(q, "dma", (out, a), [] if out[0] == "hbm" else [out], [] if a[0] == "hbm" else [a], COST["dma"] + nbytes / 250.0)
+    def asel(out, a, pat, op, cm, other=0.0):
+        rec("g", "asel", (out, a, pat, op, other, 0, cm), [out], [a], 170 + 2 * cnt(out) * COST["cyc"])
+
+    def fill(tb, n, step, base=0):
+        for k in range(0, n, 640):
+            iota(sl(tb, k, min(n, k + 640)), [[step, min(n, k + 640) - k]], base + step * k)
+
+    def dma(q, out, a, nbytes, adds=False):
+        rec(q, "dma", (out, a, adds), [] if out[0] == "hbm" else [out], [] if a[0] == "hbm" else [a],
+            COST["dma"] * (1.5 if q == "g" else 1) + nbytes / 250.0)
 
     def hbm(name, idx=None):
         return ("hbm", name, idx)
+
+    def rows(a, p, n):
+        return sl(a, 0, n, 1, slice(p, 128, 16))
 
     def gat(eng, out, win, off):
         if eng == "v":
@@ -110,140 +119,175 @@ def plan():
         else:
             act(out, ind(win, off), AF.Copy)
 
+    def times(eng, out, a, s):
+        if eng == "v":
+            ts(out, a, s, mul)
+        else:
+            act(out, a, AF.Copy, s)
+
     def zr(z, r):
         return sl(z, 15 - r, 143 - r)
 
-    def wrap(out, z, row, n, start=True):
+    def wrap(out, z, row, n, start=True, stop=True):
         for r in range(16):
-            mm(out, zr(z, r), sl(row, r, n, 16), start and r == 0, r == 15)
+            mm(out, zr(z, r), sl(row, r, n, 16), start and r == 0, stop and r == 15)
 
     add, sub, mul, mx, mn = ALU.add, ALU.subtract, ALU.mult, ALU.max, ALU.min
     band, shr = ALU.bitwise_and, ALU.arith_shift_right
     K0, K1, D0, D1, W, R, Q, U = range(8)
 
     Z = [new("b", L) for _ in range(RO + 1)]
-    X = new("b", V + L)
-    krow = new("i", 136)
-    tsi, tsb = new("i", 128), new("i", 128)
+    X = new("b", V + 2 * L)
+    kcol, tcol = new("i", 1), new("i", 1)
+    tsi = new("i", 128)
     dma("y", Z[0], hbm("zq"), 65536)
-    dma("y", sl(krow, 0, 128, 1, slice(0, 1)), hbm("kap"), 512)
-    dma("y", sl(krow, 128, 136, 1, slice(0, 1)), hbm("th"), 32)
+    dma("y", kcol, hbm("kap"), 512)
     dma("y", sl(X, 0, V), hbm("xr"), 524288)
+    iota(tcol, [[0, 1]])
+    dma("y", rows(tcol, 0, 1), hbm("th"), 32)
     for b in range(4):
         for gm in range(2):
             dma("s", sl(tsi, 32 * b + 16 * gm, 32 * b + 16 * gm + 16),
                 hbm("ts", (slice(gm, 8, 2), slice(512 * b, 512 * b + 512))), 8192)
-    dma("y", tsb, hbm("ts"), 65536)
 
     DIG = new("b", 2560)
-    ms(sl(DIG, 0, 320), 0.0)
-    for k in (320, 640, 1280):
-        act(sl(DIG, k, 2 * k), sl(DIG, 0, k), AF.Copy)
+    if OPT["dig"] == "s":
+        ms(sl(DIG, 0, 320), 0.0)
+        for k in (320, 640, 1280):
+            act(sl(DIG, k, 2 * k), sl(DIG, 0, k), AF.Copy)
+    else:
+        ms(sl(DIG, 0, 1280), 0.0)
+        act(sl(DIG, 1280, 2560), sl(DIG, 0, 1280), AF.Copy)
     pI, jrow, grow, wrow = new("i", 1), new("b", 143), new("b", 128), new("f", 16)
     iota(pI, [[0, 1]], 0, 1)
     iota(jrow, [[1, 143]])
     iota(sl(wrow, 0, 16, 2), [[1, 8]], 1)
     iota(sl(wrow, 1, 15, 2), [[-1, 7]], 7)
     iota(sl(wrow, 15, 16), [[0, 1]], 1)
-    kb = new("i", 136)
-    rec("g", "pb", (kb, sl(krow, 0, 136, 1, slice(0, 1))), [kb], [krow], 140 + 4 * 136)
     ai, mrow, negk, lw0 = new("i", 160), new("b", L), new("f", L), new("f", 16)
     iota(ai, [[1, 160]], 0, 160)
     iota(grow, [[16, 8], [0, 16]])
     iota(mrow, [[1, 16], [0, 16]])
     iota(negk, [[-1, 16], [0, 16]])
     iota(lw0, [[16, 16]], V, 1)
-    g16i, g16, pF, rcol, g15, g160, wcol, gth = [new(p, 1) for p in "ifffffff"]
+    g16i, g16, pF, rcol, g15, g160, wcol, rm16, z2c = [new(p, 1) for p in "iffffffff"]
     ts(g16i, pI, 112, band)
     cp(g16, g16i)
     cp(pF, pI)
     tt(rcol, pF, g16, sub)
     ts(g15, g16, 15.0, add)
     ts(g160, g16, 160.0, mul)
-    ts(gth, g16, 1.0 / 16, mul, 128.0, add)
+    ts(rm16, rcol, -16.0, add)
     m16, t16 = new("f", 16), new("f", 16)
     ts(m16, sl(jrow, 0, 16), rcol, ALU.is_equal)
     tt(t16, m16, wrow, mul)
     red(wcol, t16, add)
-    ZW, ZS, ZS2, ZSN, Z1 = [new("b", 143) for _ in range(5)]
+    ZW, ZS, ZS2, ZSN, ZN1, ZB, Z4, Z2 = [new("b", 143) for _ in range(8)]
+    z1c = new("f", 1)
     ts(ZW, jrow, g15, ALU.is_equal, wcol, mul)
     ts(ZS, jrow, g15, ALU.is_equal, 32768.0, mul)
-    act(ZS2, ZS, AF.Copy, 2.0)
-    act(ZSN, ZS, AF.Copy, -1.0)
-    ts(Z1, jrow, g15, ALU.is_equal, sl(m16, 0, 1), mul)
-    I1, NI, IH, INH, INQ, I2K, I16, BO, BW, DW, IX, INE, ICK, I15 = [new("b", 128) for _ in range(14)]
-    I32 = new("f", 128)
+    times(OPT["mat"], ZS2, ZS, 2.0)
+    times(OPT["mat"], ZSN, ZS, -1.0)
+    ts(z1c, sl(m16, 0, 1), -1.0, mul)
+    ts(ZN1, jrow, g15, ALU.is_equal, z1c, mul)
+    ts(ZB, jrow, g15, ALU.is_equal, sl(m16, 1, 2), mul)
+    times(OPT["mat"], Z4, ZN1, -4096.0)
+    ts(z2c, sl(m16, 1, 2), 4096.0, mul, sl(m16, 0, 1), sub)
+    ts(Z2, jrow, g15, ALU.is_equal, z2c, mul)
+    I1, NI, IH, INH, I2K, I15, I128, IN80, ICK, I3, N8, BO, BW, DW, TU, TL = [new("b", 128) for _ in range(16)]
+    I32, NI32, I32x8 = [new("f", 128) for _ in range(3)]
     crow = sl(jrow, 0, 128)
+    zer, zer32 = new("b", 640), new("f", 128)
+    iota(sl(zer, 0, 128), [[0, 128]])
+    iota(zer32, [[0, 128]])
     ts(I1, crow, pF, ALU.is_equal)
-    for t, s in ((NI, -1.0), (I2K, 2048.0), (I32, 1.0), (IH, 0.5), (INH, -0.5), (I15, 1.5), (I16, 16.0),
-                 (IX, 32.0), (INE, -0.125), (ICK, float(-CK))):
-        act(t, I1, AF.Copy, s)
+    for t, s in ((NI, -1.0), (I2K, 2048.0), (I32, 1.0)):
+        times("s", t, I1, s)
+    for t, s in ((ICK, float(-CK)), (I3, 16 * OFF * 32768), (NI32, -1.0), (IH, 0.5), (INH, -0.5), (I15, 1.5), (I128, 128.0),
+                 (IN80, -80.0), (N8, -8.0), (I32x8, 8.0)):
+        asel(t, zer32 if t[0] == "f" else sl(zer, 0, 128), [[-1, 128]], ALU.not_equal, 1, s)
     ts(BO, grow, g16, ALU.is_equal)
     ts(BW, grow, g16, ALU.is_equal, wcol, mul)
-    cidx, kidx = new("u", 16), new("u", 18)
+    asel(TU, BO, [[1, 128]], ALU.is_ge, -1)
+    asel(TL, BO, [[-1, 128]], ALU.is_gt, 1)
+    cidx = new("u", 16)
     ts(cidx, sl(jrow, 0, 16), 0.0, mul, rcol, add)
-    ts(sl(kidx, 0, 16), sl(jrow, 0, 16), g16, add)
-    ts(sl(kidx, 16, 18), sl(jrow, 0, 2), 0.0, mul, gth, add)
-    kg = new("f", 288)
-    kaprow, thc = sl(kg, 0, L), sl(kg, L, L + 1)
-    cp(kg, ind(kb, kidx))
-    LW2, LD = new("f", 32), new("f", 16)
-    LW = sl(LW2, 0, 16)
+    BO32, kf, kd, kap, tf0, thc = new("f", 128), new("f", 1), new("f", 16), new("f", 16), new("f", 1), new("f", 1)
+    ts(BO32, grow, g16, ALU.is_equal)
+    cp(kf, kcol)
+    ts(kd, m16, kf, mul)
+    mm(bank(U, 0, 16), BO32, kd, True, True)
+    act(kap, bank(U, 0, 16), AF.Copy)
+    cp(tf0, tcol)
+    mm(bank(U, 0, 1), BO32, tf0, True, True)
+    act(thc, bank(U, 0, 1), AF.Copy)
+    LW, LD, LE = new("f", 16), new("f", 16), new("f", 16)
     ts(LW, lw0, g16, sub)
-    ts(sl(LW2, 16, 32), lw0, g16, sub)
     ts(LD, LW, 256.0, add)
-    ones = new("b", L)
-    ms(ones, 1.0)
-    half, thr, big0, big, pw16, pcol = new("f", L), new("b", L), new("f", 1), new("f", 1), new("f", 16), new("f", 1)
+    ts(LE, LW, 255.0, add)
+    ones, noff, c4k, c16, gap = new("b", L), new("b", L), new("b", 16), new("b", 128), new("b", 160)
+    iota(ones, [[0, L]], 1)
+    iota(noff, [[0, L]], -int(OFF))
+    iota(c4k, [[0, 16]], 4096)
+    iota(c16, [[0, 128]], 16)
+    iota(gap, [[0, 160]], -256)
+    iota(sl(zer, 128, 640), [[0, 512]])
+    half, thr, big0, big, pw16, pcol = new("b", L), new("b", L), new("f", 1), new("f", 1), new("f", 16), new("f", 1)
     ms(half, 0.5)
     ms(sl(half, 0, L, 16), 1.0)
     ms(big0, 2.0 ** 60)
     ts(big, big0, 2.0 ** 61, mul)
-    scan(thr, half, negk, big, mul, mx)
+    scan(thr, half, sl(zer, 0, L), big, mul, mx)
     tt(pw16, sl(thr, 0, 16), m16, mul)
     red(big0, pw16, add)
     ts(pcol, big0, 2.0 ** -50, mul, 2.0 ** -50, mul)
     ts(DW, grow, g16, ALU.is_equal, pcol, mul)
 
-    def digits(src, n, table, q):
-        loi, hii, lo, hi = new("i", n), new("i", n), new("b", n), new("b", n)
-        ts(loi, src, 15, band)
-        ts(hii, src, 4, shr)
-        cp(lo, loi)
-        ts(hi, hii, 2.0, mul)
-        dma(q, sl(table, 0, 16 * n, 1, slice(0, 128, 16)), lo, 256 * n)
-        dma(q, sl(table, 0, 16 * n, 1, slice(14, 128, 16)), hi, 256 * n)
-
-    ab = new("i", 160)
+    ab, loi, hii, lo, hi = new("i", 160), new("i", 160), new("i", 160), new("b", 160), new("b", 160)
     ts(ab, ai, g160, sub)
-    digits(ab, 160, DIG, "y")
-    TD = [new("b", V + L) for _ in range(RO)] + [new("b", V)]
-    iota(sl(TD[0], 0, V), [[0, V]])
-    digits(tsb, 128, TD[0], "y")
+    ts(loi, ab, 15, band)
+    ts(hii, ab, 4, shr)
+    ts(lo, loi, 1 / FR, mul)
+    ts(hi, hii, 2 / FR, mul)
+    dma("y", rows(DIG, 0, 2560), lo, 40960)
+    dma("y", rows(DIG, 14, 2560), hi, 40960)
+    XT = [new("f", 2560), new("f", 2560)]
+    dma("g", sl(XT[1], 0, V), hbm("xr"), 1048576)
+    for p in (0, 14):
+        dma("g", rows(XT[1], p, V), rows(DIG, p, V), 65536, True)
     G = [new("b", 2560) for _ in range(RO)]
     M = [new("b", 2560) for _ in range(RO)]
     CU = [new("b", 2560) for _ in range(RO)]
+    GW = [2560, 2320, 2320]
+    IOT, TS = new("f", V), new("f", V)
     for t in range(RO):
-        for tb, n in ((G[t], 2560 if t == 0 else 2320), (M[t], V)):
-            for k in range(0, n, 640):
-                iota(sl(tb, k, min(n, k + 640)), [[0, min(n, k + 640) - k]])
+        fill(G[t], GW[t], 0)
+        dma("y", rows(G[t], 1, GW[t]), sl(gap, 0, GW[t] // 16), 16 * GW[t])
+        fill(M[t], V, 0)
+    fill(IOT, V, 1)
     tsf, tst, tsw = new("f", 128), new("f", 128), new("u", 128)
     cp(tsf, tsi)
     rec("v", "tr", (tst, tsf), [tst], [tsf], 128 * COST["cyc"])
     cp(tsw, tst)
     PD = new("b", V + L)
     phase[0] = "b"
-    for k in range(8):
-        cp(ind(sl(PD, 0, V), sl(tsw, 16 * k, 16 * k + 16)), sl(DIG, 256 * k, 256 * k + 256))
-    XT = [new("b", 2560), new("b", 2560)]
+    n = 128 // OPT["pd"]
+    for k in range(0, 128, n):
+        cp(ind(sl(PD, 0, V), sl(tsw, k, k + n)), sl(DIG, 16 * k, 16 * (k + n)))
+    phase[0] = "c"
+    n = 128 // len(OPT["x0"])
+    for k, e in enumerate(OPT["x0"]):
+        o, a = sl(XT[0], 16 * n * k, 16 * n * (k + 1)), ind(sl(XT[1], 0, V), sl(tsw, n * k, n * (k + 1)))
+        if e == "v":
+            ts(o, a, OFF, add)
+        else:
+            act(o, a, AF.Identity, 1.0, OFF)
 
     def regather(out, win, off, engs):
         n = 128 // len(engs)
         for k, e in enumerate(engs):
             gat(e, sl(out, 16 * n * k, 16 * n * (k + 1)), win, sl(off, n * k, n * (k + 1)))
 
-    phase[0] = "c"
-    regather(XT[0], sl(X, 0, V), tsw, OPT["xt"][0])
     colA, thA, thK = new("f", 1), new("f", 1), new("f", 1)
     ms(colA, -13.0)
     thB, thL = new("f", 1), new("f", 1)
@@ -253,12 +297,17 @@ def plan():
     ts(thL, thc, 128.0 - 509.0, add, 32768.0, mul)
 
     DT, AB = new("b", 16 * L), new("b", 16 * L)
-    SH = new("b", V)
     EQ = [new("b", 2176), new("b", 2176)]
     dbank = [0]
 
-    def nearest(units, win, off, zrow, h32, centre):
-        for lo, hi in OPT["sum"]:
+    def nearest(units, win, off, zrow, low, nodes):
+        o0 = OFF if nodes else 0.0
+        acc, groups, lo = None, [], 0
+        for part in units.split():
+            groups.append((lo, lo + len(part)))
+            lo += len(part)
+        units = "".join(units.split())
+        for gi, (lo, hi) in enumerate(groups):
             m = lo
             while m < hi:
                 e = m
@@ -271,54 +320,63 @@ def plan():
                     dbank[0] += 1
                     for j in range(m, e):
                         o = bank(bk, L * (j - m), L * (j - m + 1))
-                        mm(o, I1, sl(DT, L * j, L * j + L), True, False)
-                        mm(o, NI, zrow, False, True)
-                    act(a, bank(bk, 0, L * (e - m)), AF.Abs)
+                        mm(o, NI, zrow, True, False)
+                        mm(o, I1, sl(DT, L * j, L * j + L), False, True)
+                    act(a, bank(bk, 0, L * (e - m)), AF.Abs, 1.0, -o0)
                 else:
                     for j in range(m, e):
                         tt(sl(DT, L * j, L * j + L), ind(win, sl(off, 16 * j, 16 * j + 16)), zrow, sub)
                     if units[m] == "A":
-                        act(a, d, AF.Abs)
+                        act(a, d, AF.Abs, 1.0, -o0)
                     else:
-                        ts(a, d, 0.0, mx)
+                        ts(a, d, o0, mx, -o0, add)
                 m = e
-            bk, base = (K0, 0) if lo < 8 else (K1, 8)
-            whole = bank(bk, 16 * (lo - base), 16 * (hi - base))
-            mm(whole, I2K, sl(mrow, 16 * lo, 16 * hi), True, False)
-            if centre:
-                mm(whole, ICK, sl(ones, 16 * lo, 16 * hi), False, False)
+            bk = (K0, K1)[gi & 1]
+            w = 16 * (hi - lo)
+            whole = bank(bk, 0, w)
+            if nodes:
+                mm(whole, I2K, sl(ones, 0, w), True, False)
+                mm(whole, ICK, sl(ones, 0, w), False, False)
+            else:
+                mm(whole, I2K, sl(mrow, 16 * lo, 16 * hi), True, False)
             last = "B" in units[lo:hi]
+            il = NI32 if nodes else I32
             if not last:
-                mm(whole, I32, sl(h32, 16 * lo, 16 * hi), False, False)
+                mm(whole, il, sl(low, 16 * lo, 16 * hi), False, False)
             m = lo
             while m < hi:
                 e = m
                 while e < hi and (units[e] == "B") == (units[m] == "B"):
                     e += 1
-                o = bank(bk, 16 * (m - base), 16 * (e - base))
-                for r in range(16):
-                    if units[m] == "B":
+                o = bank(bk, 16 * (m - lo), 16 * (e - lo))
+                if units[m] == "B":
+                    if nodes:
+                        mm(o, I3, sl(ones, 0, 16 * (e - m)), False, False)
+                    for r in range(16):
                         mm(o, zr(ZSN, r), sl(DT, L * m + r, L * e, 16), False, False)
                 for r in range(16):
                     mm(o, zr(ZS2 if units[m] == "B" else ZS, r), sl(AB, L * m + r, L * e, 16), False, e == hi and r == 15 and not last)
                 m = e
             if last:
-                mm(whole, I32, sl(h32, 16 * lo, 16 * hi), False, True)
-        k0, k1, k2, k3, key = new("f", 128), new("f", 128), new("f", 64), new("f", 32), new("i", 16)
-        act(k0, bank(K0, 0, 128), AF.Copy)
-        tt(k1, bank(K1, 0, 128), k0, mn)
-        tt(k2, sl(k1, 0, 64), sl(k1, 64, 128), mn)
-        tt(k3, sl(k2, 0, 32), sl(k2, 32, 64), mn)
-        tt(key, sl(k3, 0, 16), sl(k3, 16, 32), mn)
-        vi, vu = new("i", 16), new("u", 16)
-        ts(vi, key, V - 1, band)
-        cp(vu, vi)
-        return key, vi, vu
+                mm(whole, il, sl(low, 16 * lo, 16 * hi), False, True)
+            nxt = new("i" if w == 16 and hi == 16 else "f", w)
+            if acc is None:
+                act(nxt, whole, AF.Copy)
+            else:
+                tt(nxt, whole, acc, mn)
+            acc = nxt
+            goal = 16 * (groups[gi + 1][1] - hi) if hi < 16 else 16
+            while w > goal:
+                w //= 2
+                nxt = new("i" if w == 16 and hi == 16 else "f", w)
+                tt(nxt, sl(acc, 0, w), sl(acc, w, 2 * w), mn)
+                acc = nxt
+        return acc
 
-    def firsts(dig, kw, miss, eq, bk):
+    def firsts(dig, kw, miss, eq, bk, spare, flag=None):
         kr, km, fr, fw = new("u", L), new("f", 16), new("b", L), new("f", 16)
         mm(bank(Q, 256, 512), BW, dig, True, True)
-        cp(kr, bank(Q, 256, 512))
+        ts(kr, bank(Q, 256, 512), FR, mul)
         tt(km, kw, miss, add)
         mm(bank(Q, 0, L), NI, thr, True, False)
         o = 0
@@ -328,209 +386,226 @@ def plan():
             mm(bank(Q, 16 * c, L), DW, sl(eq, o, o + n), False, c == 15)
             o += n
         act(fr, bank(Q, 0, L), AF.Sign)
-        wrap(bank(bk, 0, 16), Z1, fr, L)
-        ts(fw, bank(bk, 0, 16), 0.0, ALU.is_lt)
+        y = bank(bk, 0, 16)
+        mm(y, I1, c4k, True, False)
+        mm(y, I1, miss, False, False)
+        if flag:
+            wrap(y, flag[0], flag[1], L, False, False)
+        wrap(y, Z4, fr, L, False)
+        tt(fw, y, spare, mn)
         return fw
 
     ci, hi_, tf, h32 = new("i", L), new("i", L), new("f", L), new("f", L)
-    atf, a32, tg = new("f", L), new("f", L), new("f", L)
+    atf, tg = new("f", L), new("f", L)
     for t in range(RO):
-        z, xt = Z[t], sl(XT[t & 1], 0, V)
+        z, xt, final = Z[t], sl(XT[t & 1], 0, V), t + 1 == RO
         phase[0] = "h%d" % t
         u2, sq, a2, hu = new("f", 16), new("f", 16), new("i", 16), new("u", L)
         wrap(bank(W, 0, 16), ZW, z, L)
         cp(u2, bank(W, 0, 16))
         tt(sq, bank(W, 0, 16), u2, mul)
         ts(a2, sq, colA, add, 1.0 / 32, mul)
-        for lo, hi in OPT["cut1"]:
+        for lo, hi in OPT["cut"]:
             a, b = 16 * lo, 16 * hi
-            if (lo, hi) in OPT["tf_s"]:
-                for m in range(lo, hi):
-                    act(sl(tf, 16 * m, 16 * m + 16), u2, AF.Copy, sl(kaprow, 16 * m, 16 * m + 1))
-            else:
-                tt(sl(tf, a, b), ind(u2, sl(cidx, lo, hi)), sl(kaprow, a, b), mul)
+            for m in range(lo, hi):
+                times("v" if m < OPT["tf"][t] else "s", sl(tf, 16 * m, 16 * m + 16), u2, sl(kap, m, m + 1))
             tt(sl(ci, a, b), ind(a2, sl(cidx, lo, hi)), sl(tf, a, b), add)
             ts(sl(hi_, a, b), sl(ci, a, b), V - 1, band)
             cp(sl(hu, a, b), sl(hi_, a, b))
             ts(sl(h32, a, b), sl(hi_, a, b), float(-CK), add)
         phase[0] = "s%d" % t
-        key, si, su = nearest(UNITS[(t, 0)], sl(X, 0, V), hu, z, h32, False)
+        key = nearest(UNITS[(t, 0)], sl(X, 0, V), hu, z, h32, False)
+        si, su = new("i", 16), new("u", 16)
+        ts(si, key, V - 1, band)
+        cp(su, si)
         phase[0] = "m%d" % t
         xp = new("b", 2 * L)
         xs, pd = sl(xp, 0, L), sl(xp, L, 2 * L)
-        gat("v", xs, sl(X, 0, V), su)
+        gat(OPT["xs"][t], xs, sl(X, 0, V), su)
         gat("s", pd, sl(PD, 0, V), su)
         wrap(bank(W, 0, 32), ZW, xp, 2 * L)
-        i2, dm, d2, au = new("i", 32), new("i", 16), new("f", 16), new("u", L)
-        cp(i2, bank(W, 0, 32))
-        tau = p = sl(i2, 16, 32)
+        i2, dm, d2, au = new("i", 16), new("i", 16), new("f", 16), new("u", L)
+        tau = p = new("f", 16)
+        pu = new("u", 16)
+        if t:
+            ts(pu, bank(W, 16, 32), FR, mul)
+        cp(i2, bank(W, 0, 16))
+        ts(tau, bank(W, 16, 32), FR, mul)
         for k in range(t):
-            pu, cg, p2 = new("u", 16), new("b", L), new("f", 16)
-            cp(pu, p)
-            gat(OPT["link"], cg, sl(CU[k], 0, 2560 if k == 0 else 2320), pu)
-            wrap(bank(W, 0, 16), Z1, cg, L)
-            tt(p2, p, bank(W, 0, 16), sub)
+            cg, p2 = new("b", L), new("f", 16)
+            gat(OPT["link"][t + k - 1], cg, sl(CU[k], 0, GW[k]), pu)
+            mm(bank(W, 0, 16), I32, p, True, False)
+            wrap(bank(W, 0, 16), ZN1, cg, L, False)
+            if k + 1 < t:
+                pu = new("u", 16)
+                cp(pu, bank(W, 0, 16))
+            cp(p2, bank(W, 0, 16))
             p = p2
-        ts(dm, sl(i2, 0, 16), 15, band)
+        ts(dm, i2, 15, band)
         ts(d2, dm, 1.0, add)
-        for lo, hi in OPT["cut2"]:
-            a, b = 16 * lo, 16 * hi
-            if (lo, hi) in OPT["tg_s"][min(t, 1)]:
-                for m in range(lo, hi):
-                    act(sl(tg, 16 * m, 16 * m + 16), d2, AF.Copy, float(-m))
+        for c in range(16 if OPT["at"][t] >= 0 else 0):
+            o, ks, dc, pc = sl(atf, c, L, 16), sl(negk, 0, L, 16), sl(d2, c, c + 1), sl(p, c, c + 1)
+            if c < OPT["at"][t]:
+                ts(o, ks, dc, mul, pc, add)
             else:
-                tt(sl(tg, a, b), ind(d2, sl(cidx, lo, hi)), sl(negk, a, b), mul)
-            tt(sl(atf, a, b), ind(p, sl(cidx, lo, hi)), sl(tg, a, b), add)
+                act(o, ks, AF.Identity, dc, pc)
+        for lo, hi in OPT["cut"]:
+            a, b = 16 * lo, 16 * hi
+            if OPT["at"][t] < 0:
+                if lo and OPT["at"][t] == -2:
+                    for m in range(lo, hi):
+                        act(sl(tg, 16 * m, 16 * m + 16), d2, AF.Copy, float(-m))
+                else:
+                    tt(sl(tg, a, b), ind(d2, sl(cidx, lo, hi)), sl(negk, a, b), mul)
+                tt(sl(atf, a, b), ind(p, sl(cidx, lo, hi)), sl(tg, a, b), add)
             ts(sl(au, a, b), sl(atf, a, b), -1.0, add)
-            act(sl(a32, a, b), sl(atf, a, b), AF.Relu, 1.0, -1.0)
         phase[0] = "p%d" % t
-        hitw, miss = new("f", 16), new("f", 16)
-        ts(hitw, key, thK, ALU.is_lt)
-        ts(miss, key, thK, ALU.is_ge, 4096.0, mul)
-        adz, sgn, sg, zh, cc, vs, dz, v0 = [new("b", L) for _ in range(8)]
+        miss = new("b", 16)
+        ts(miss, key, thK, ALU.is_ge, 8192.0, mul)
+        adz, sgn, cc, dz, vs = [new("b", L) for _ in range(5)]
         mm(bank(U, 0, L), I1, z, True, False)
         mm(bank(U, 0, L), NI, xs, False, True)
         act(adz, bank(U, 0, L), AF.Abs)
-        act(dz, bank(U, 0, L), AF.Copy)
-        ts(cc, dz, -2.0, mx, 2.0, mn)
+        if OPT["cc"][t] == "s":
+            act(dz, bank(U, 0, L), AF.Copy)
+            ts(cc, dz, -2.0, mx, 2.0, mn)
+        else:
+            ts(cc, bank(U, 0, L), -2.0, mx, 2.0, mn)
         mm(bank(U, L, 2 * L), BO, adz, True, True)
         nsum = new("f", 1)
-        act(sgn, bank(U, L, 2 * L), AF.Sign, -1.0, thA, nsum)
-        mm(bank(U, 0, L), I1, z, True, False)
-        mm(bank(U, 0, L), IX, sgn, False, True)
-        act(zh, bank(U, 0, L), AF.Relu, 1.0, -32.0)
+        act(sgn, bank(U, L, 2 * L), AF.Sign, -1.0, thA, None if final else nsum)
         mm(bank(U, 0, L), IH, z, True, False)
         mm(bank(U, 0, L), IH, xs, False, True)
-        act(v0, bank(U, 0, L), AF.Identity, 1.0, 159.75)
-        vs = sl(XT[t & 1], V, V + L)
-        ts(vs, v0, -160.0, add)
-        if t + 1 < RO:
+        act(vs, bank(U, 0, L), AF.Identity, 1.0, OFF - 0.25)
+        if not final:
             colA, thA, thK = new("f", 1), new("f", 1), new("f", 1)
             act(colA, nsum, AF.Identity, -16.0, 4083.0)
             act(thA, nsum, AF.Identity, -0.5, thB)
             act(thK, nsum, AF.Identity, -16384.0, thL)
+        else:
+            phase[0] = "k"
+            cf, cr, ids = new("f", 256), new("b", 256), new("f", 128)
+            dma("y", sl(cf, 0, 128), rows(xt, 0, V), 65536)
+            dma("y", sl(cf, 128, 256), rows(xt, 14, V), 65536)
+            act(cr, cf, AF.Copy)
+            mm(bank(U, 0, 128), I32, sl(cf, 0, 128), True, False)
+            mm(bank(U, 0, 128), I32x8, sl(cf, 128, 256), False, False)
+            mm(bank(U, 0, 128), NI, sl(cr, 0, 128), False, False)
+            mm(bank(U, 0, 128), N8, sl(cr, 128, 256), False, True)
+            act(ids, bank(U, 0, 128), AF.Copy, FR)
+            dma("y", rows(XT[1 - (t & 1)], 0, V), ids, 65536)
         phase[0] = "d%d" % t
-        dd, okw, t32, q32, uu = new("f", 32), new("f", 16), new("f", 32), new("f", 32), new("u", 48)
-        tt(sl(dd, 0, 16), si, LW, sub)
-        tt(sl(dd, 16, 32), p, LW, sub)
-        fs = firsts(pd, tau, miss, EQ[0], U)
-        tt(okw, fs, hitw, mul)
-        tt(sl(t32, 0, 16), sl(dd, 0, 16), okw, mul)
-        tt(sl(t32, 16, 32), sl(dd, 16, 32), okw, mul)
-        tt(q32, t32, LW2, add)
+        q32, uu = new("f", 32), new("u", 48)
+        fs = firsts(pd, tau, miss, EQ[0], U, LW)
+        tt(sl(q32, 0, 16), fs, si, mx)
+        tt(sl(q32, 16, 32), fs, p, mx)
         q, sou, qu = sl(q32, 16, 32), sl(uu, 0, 16), sl(uu, 16, 48)
         cp(sl(uu, 0, 32), q32)
         ts(sl(uu, 32, 48), q, 1.0, add)
-        gat("s", sl(TD[t], V, V + L), sl(DIG, 0, V), su)
         phase[0] = "x%d" % t
-        cp(ind(X, sou), vs)
-        if t + 1 < RO:
+        tt(ind(X, sou), vs, noff, add)
+        if final:
+            gat("s", sl(XT[1 - (t & 1)], V, V + L), IOT, su)
+        else:
+            if OPT["app"][t] == "v":
+                tt(sl(XT[t & 1], V, V + L), ind(sl(DIG, 0, V), su), vs, add)
+            else:
+                sd = new("b", L)
+                gat("s", sd, sl(DIG, 0, V), su)
+                mm(bank(U, 0, L), I1, vs, True, False)
+                mm(bank(U, 0, L), I1, sd, False, True)
+                act(sl(XT[t & 1], V, V + L), bank(U, 0, L), AF.Copy)
             cp(ind(PD, sou), sl(DIG, V + L * t, V + L * t + L))
         phase[0] = "o%d" % t
-        gw = 2560 if t == 0 else 2320
+        gw = GW[t]
         cp(ind(sl(G[t], 0, V + L), sl(qu, 0, 16)), ones)
         for k in range(0, gw, 640):
             e = min(gw, k + 640)
-            scan(sl(CU[t], k, e), sl(G[t], k, e), sl(G[t], k, e), 0.0 if k == 0 else sl(CU[t], k - 1, k), add, mx)
-        cg, cw, fl, t1, a1, ps, pu = new("b", 2 * L), new("f", 32), new("f", 16), new("f", 16), new("f", 16), new("f", 16), new("u", 16)
+            scan(sl(CU[t], k, e), sl(G[t], k, e), sl(zer, 0, e - k), 0.0 if k == 0 else sl(CU[t], k - 1, k), add, mx)
+        cg, ps, pu, dw, of, ou = new("b", 2 * L), new("f", 16), new("u", 16), new("b", 128), new("f", 128), new("u", 128)
         gat("s", cg, sl(CU[t], 0, gw), qu)
-        wrap(bank(U, 0, 32), Z1, cg, 2 * L)
-        act(cw, bank(U, 0, 32), AF.Identity, 1.0, -1.0)
-        tt(fl, sl(cw, 16, 32), sl(cw, 0, 16), sub)
-        tt(a1, q, sl(cw, 16, 32), sub)
-        tt(t1, fl, LD, mul)
-        tt(ps, t1, a1, mx)
-        cp(pu, ps)
-        cp(ind(M[t], pu), sl(cg, L, 2 * L))
-        for k in range(0, V, 512):
-            scan(sl(SH, k, k + 512), sl(M[t], k, k + 512), sl(M[t], k, k + 512), 0.0 if k == 0 else sl(SH, k - 1, k), mx, mx)
-        ou = new("u", 128)
-        for k in (0, 64):
-            mm(bank(U, k, k + 64), I16, sl(jrow, k, k + 64), True, False)
-            wrap(bank(U, k, k + 64), Z1, sl(SH, 16 * k, 16 * k + 1024), 1024, False)
-            ts(sl(ou, k, k + 64), bank(U, k, k + 64), rcol, add)
-        phase[0] = "t%d" % t
-        regather(TD[t + 1], TD[t], ou, OPT["td"][t])
-        if t + 1 < RO and OPT["xe"][t] == "y":
-            pass
-        elif t + 1 < RO:
-            tw = new("u", 128)
-            for k in (0, 64):
-                wrap(bank(U, k, k + 64), ZW, sl(TD[t + 1], 16 * k, 16 * k + 1024), 1024)
-                cp(sl(tw, k, k + 64), bank(U, k, k + 64))
-        else:
-            for r in range(16):
-                mm(bank(U, 0, 128), zr(ZW, r), sl(TD[t + 1], 128 * r, 128 * r + 128), r == 0, r == 15)
-            act(tst, bank(U, 0, 128), AF.Copy)
-            dma("s", hbm("yt"), tst, 65536)
+        mm(bank(U, 0, 16), I32, q, True, False)
+        wrap(bank(U, 0, 16), Z2, sl(cg, L, 2 * L), L, False)
+        tt(ps, bank(U, 0, 16), LE, mn)
+        ts(pu, ps, 1.0, add)
+        cp(ind(M[t], pu), sl(cg, 0, L))
+        wrap(bank(U, 0, 128), ZB, M[t], V)
+        act(dw, bank(U, 0, 128), AF.Copy)
+        mm(bank(U, 0, 128), TU, dw, True, False)
+        mm(bank(U, 1, 128), TL, sl(dw, 0, 127), False, True)
+        scan(of, bank(U, 0, 128), c16, rm16, add, add)
+        cp(ou, of)
+        if final:
+            phase[0] = "t"
+            regather(TS, sl(XT[1 - (t & 1)], 0, V + L), ou, OPT["xt"][t])
+            for k in (0, V // 2):
+                dma("y", hbm("yt", (slice(0, 8), slice(k, k + V // 2))), rows(sl(TS, k, k + V // 2), 0, V // 2), 32768)
         phase[0] = "n%d" % t
-        _, ni, nu = nearest(UNITS[(t, 1)], xt, au, xs, a32, True)
+        keyn = nearest(UNITS[(t, 1)], xt, au, xs, atf, True)
+        ni, nu = new("i", 16), new("u", 16)
+        ts(ni, keyn, 4095, band)
+        ts(nu, ni, -1.0, mul, 2047.0, add)
         phase[0] = "z%d" % t
-        tz, av, zs, ng = new("b", L), new("b", L), new("b", L), new("b", 2 * L)
-        nd = sl(ng, 0, L)
+        xn, tz, zs = new("b", L), new("b", L), new("b", L)
+        mm(bank(W, 0, L), INH, z, True, False)
+        mm(bank(W, 0, L), I128, sgn, False, False)
         mm(bank(R, 0, L), I1, z, True, False)
-        mm(bank(R, 0, L), INH, zh, False, False)
-        mm(bank(R, 0, L), INE, sgn, False, False)
-        vn0 = new("b", L)
+        mm(bank(R, 0, L), IN80, sgn, False, False)
+        gat(OPT["vn0"][t], xn, xt, nu)
+        mm(bank(W, 0, L), I15, xn, False, True)
+        mm(bank(R, 0, L), NI, xn, False, False)
         if OPT["tz"][t] == "v":
-            act(sg, sgn, AF.Identity, 0.75, -0.25)
-            tt(tz, ind(xt, nu), sg, mul)
-            mm(bank(R, 0, L), I1, tz, False, True)
+            ts(tz, bank(W, 0, L), 31.75 - 1.5 * OFF, add, 0.0, mx)
         else:
-            gat("s", vn0, xt, nu)
-            mm(bank(W, 0, L), IX, sgn, True, False)
-            mm(bank(W, 0, L), I1, vn0, False, True)
-            act(tz, bank(W, 0, L), AF.Relu, 1.0, -32.0)
-            mm(bank(R, 0, L), NI, vn0, False, False)
-            mm(bank(R, 0, L), I15, tz, False, True)
-        act(av, bank(R, 0, L), AF.Abs, 1.0, -0.125)
-        ts(zs, av, MAGIC, add, -MAGIC, add)
+            act(tz, bank(W, 0, L), AF.Relu, 1.0, 31.75 - 1.5 * OFF)
+        mm(bank(R, 0, L), I1, tz, False, True)
+        act(zs, bank(R, 0, L), AF.Abs, 1.0, OFF - 80.0)
         rec("g", "send", (t, zs, Z[t + 1]), [], [zs], 600)
         rec("s", "own", (t, zs, Z[t + 1]), [Z[t + 1]], [zs], 64)
         rec("x", "arr", (t, len(ops) - 2), [Z[t + 1]], [], COST["rem"])
         phase[0] = "e%d" % t
-        gat("s", nd, sl(TD[t], 0, V), nu)
-        gat("s", sl(ng, L, 2 * L), sl(G[t], 0, V), nu)
-        nw, vn, nou, hk = new("f", 32), new("b", L), new("u", 16), new("f", 16)
-        wrap(bank(W, 0, 32), ZW, ng, 2 * L)
-        act(nw, bank(W, 0, 32), AF.Copy)
-        dn, de, tn, on = [new("f", 16) for _ in range(4)]
-        tt(hk, hitw, sl(nw, 16, 32), ALU.is_gt)
-        tt(dn, sl(nw, 0, 16), LW, sub)
-        tt(de, dn, hk, mul)
-        fn = firsts(nd, sl(nw, 0, 16), miss, EQ[1], W)
-        tt(tn, de, fn, mul)
-        tt(on, tn, LW, add)
-        v1, v2 = new("b", L), new("b", L)
-        if OPT["vn"][t] == "v":
-            tt(v1, ind(xt, nu), cc, add)
-            ts(vn, v1, 0.0, mx, 63.0, mn)
+        nd, nw, vn, ng, qn, un = new("b", L), new("f", 16), new("b", L), new("b", L), new("f", 32), new("u", 32)
+        if OPT["nd"][t] == "v":
+            tt(nd, ind(xt, nu), xn, sub)
         else:
-            if OPT["tz"][t] == "v":
-                gat("s", vn0, xt, nu)
-            mm(bank(R, 0, L), I1, cc, True, False)
-            mm(bank(R, 0, L), I1, vn0, False, True)
-            act(v1, bank(R, 0, L), AF.Relu)
-            if OPT["vn"][t] == "s":
-                ts(vn, v1, 63.0, mn)
-            else:
-                act(v2, v1, AF.Relu, -1.0, 63.0)
-                act(vn, v2, AF.Identity, -1.0, 63.0)
-        cp(nou, on)
-        cp(ind(X, nou), vn)
-        if t + 1 < RO and OPT["xe"][t] == "y":
-            d3, e3, t3, o3, u3 = new("f", 16), new("f", 16), new("f", 16), new("f", 16), new("u", 16)
-            tt(d3, ni, LD, sub)
-            tt(e3, d3, hk, mul)
-            tt(t3, e3, fn, mul)
-            tt(o3, t3, LD, add)
-            cp(u3, o3)
-            cp(ind(XT[t & 1], u3), vn)
+            wn = new("f", L)
+            gat("s", wn, xt, nu)
+            mm(bank(R, 0, L), NI, xn, True, False)
+            mm(bank(R, 0, L), I32, wn, False, True)
+            act(nd, bank(R, 0, L), AF.Copy)
+        gat("s", ng, sl(G[t] if final else CU[t], 0, V), nu)
+        wrap(bank(W, 0, 16), ZW, nd, L)
+        act(nw, bank(W, 0, 16), AF.Copy, FR)
+        nf, n2, keys = new("f", 16), new("f", 16), (nd, nw)
+        if not final or OPT["ek"][t] != "i":
+            cp(nf, nu)
+        if OPT["ek"][t] != "i":
+            keys = (new("b", L), nf)
+            gat(OPT["ek"][t], keys[0], sl(DIG, 0, V), nu)
+        fn = firsts(keys[0], keys[1], miss, EQ[1], W, LD, (Z4 if final else Z2, ng))
+        if not final:
+            tt(n2, bank(W, 0, 16), nf, add)
+            tt(sl(qn, 16, 32), n2, LD, mn)
+        tt(sl(qn, 0, 16), fn, nw, mx)
+        mm(bank(R, 0, L), I1, cc, True, False)
+        mm(bank(R, 0, L), I1, xn, False, True)
+        if OPT["vn"][t] == "v":
+            ts(vn, bank(R, 0, L), OFF, mx, OFF + 63.0, mn)
+        else:
+            v1 = new("b", L)
+            act(v1, bank(R, 0, L), AF.Relu, 1.0, -OFF)
+            ts(vn, v1, 63.0, mn, OFF, add)
+        cp(sl(un, 0, 16), sl(qn, 0, 16))
+        tt(ind(X, sl(un, 0, 16)), vn, noff, add)
+        if not final:
             phase[0] = "r%d" % t
-            regather(XT[(t + 1) & 1], sl(XT[t & 1], 0, V + L), ou, OPT["xt"][t + 1])
-        elif t + 1 < RO:
-            phase[0] = "r%d" % t
-            regather(XT[(t + 1) & 1], sl(X, 0, V), tw, OPT["xt"][t + 1])
+            vx = new("f", L)
+            regather(XT[(t + 1) & 1], sl(XT[t & 1], 0, V + L), ou, OPT["xt"][t])
+            mm(bank(R, 0, L), I1, vn, True, False)
+            mm(bank(R, 0, L), I1, nd, False, True)
+            act(vx, bank(R, 0, L), AF.Copy)
+            cp(sl(un, 16, 32), sl(qn, 16, 32))
+            cp(ind(XT[(t + 1) & 1], sl(un, 16, 32)), vx)
     dma("y", hbm("yx"), sl(X, 0, V), 524288)
     dma("s", hbm("yz"), Z[RO], 65536)
     return ops, top
@@ -552,111 +627,142 @@ def depend(ops):
                 h = hist.setdefault((a[0], a[5]), [])
                 keep = []
                 for e in h:
-                    hitx = e[0] < hi and lo < e[1]
+                    hitx = e[0] < hi and lo < e[1] and (a[4] is None or e[4] is None or a[4].start == e[4].start)
+                    if a[3] == e[5] and (lo - e[0]) % a[3]:
+                        hitx = False
                     if hitx and (w or e[2]) and e[3] != i and not (o["m"] == "arr" and ops[e[3]]["m"] == "own"):
                         d.add(e[3])
-                    if not (w and lo <= e[0] and e[1] <= hi and o["m"] != "arr"):
+                    if not (w and lo <= e[0] and e[1] <= hi and o["m"] != "arr" and a[4] is None and a[3] == 1):
                         keep.append(e)
-                keep.append((lo, hi, w, i))
+                keep.append((lo, hi, w, i, a[4], a[3]))
                 hist[(a[0], a[5])] = keep
         deps.append(d)
     return deps
 
 
 def schedule(ops, deps=None):
-    n = len(ops)
     deps = depend(ops) if deps is None else deps
-    succ = [[] for _ in range(n)]
-    for i in range(n):
-        for j in deps[i]:
-            succ[j].append(i)
+    job, jobs = [0] * len(ops), []
+    for i, o in enumerate(ops):
+        if o["e"] == "t" and ops[i - 1]["e"] == "t" and o["a"][0][0] == ops[i - 1]["a"][0][0] and len(jobs[-1][0]) < OPT["run"] and \
+                all(job[j] == job[i - 1] or job[j] in jobs[-1][1] for j in deps[i]):
+            jobs[-1][0].append(i)
+        else:
+            jobs.append(([i], {job[j] for j in deps[i]}))
+        job[i] = len(jobs) - 1
+    n = len(jobs)
+    eng = [ops[m[0]]["e"] for m, d in jobs]
+    kind = [ops[m[0]]["m"] for m, d in jobs]
+    cost = [sum(ops[i]["c"] for i in m) for m, d in jobs]
+    hold = [(1000.0 if eng[k] == "g" else 60.0) if kind[k] == "dma" else (0.0 if kind[k] == "arr" else cost[k]) for k in range(n)]
 
     def lag(j, i):
-        if ops[j]["e"] == ops[i]["e"] and ops[j]["m"] != "dma":
-            return 0.0 if ops[i]["e"] == "t" else COST["self"]
+        if eng[j] == eng[i] and kind[j] != "dma":
+            return 0.0 if eng[i] == "t" else COST["self"]
         return COST["hop"]
 
-    lvl = [0.0] * n
-    for i in range(n - 1, -1, -1):
-        lvl[i] = ops[i]["c"] + max([lvl[k] + lag(i, k) for k in succ[i]] + [0.0])
-    cost = [o["c"] for o in ops]
-    hold = [60.0 if o["m"] == "dma" else (0.0 if o["m"] == "arr" else o["c"]) for o in ops]
-    pre = [[(j, lag(j, i)) for j in deps[i]] for i in range(n)]
-    post = [[(k, lag(i, k)) for k in succ[i]] for i in range(n)]
+    pre = [[(j, lag(j, i)) for j in jobs[i][1]] for i in range(n)]
+    post = [[] for _ in range(n)]
+    for i in range(n):
+        for j, l in pre[i]:
+            post[j].append((i, l))
 
     def place(seq, before, back):
-        busy = {e: ([], []) for e in "vstgyx"}
-        start, end = [0.0] * n, [0.0] * n
+        busy = {e: ([], [], []) for e in "vstgyx"}
+        start, end, why = [0.0] * n, [0.0] * n, [-1] * n
         for i in seq:
-            t = 0.0
+            t, w = 0.0, -1
             for j, l in before[i]:
                 if end[j] + l > t:
-                    t = end[j] + l
+                    t, w = end[j] + l, j
             off = cost[i] - hold[i] if back else 0.0
             t += off
             h = hold[i]
             if h:
-                bs, be = busy[ops[i]["e"]]
-                lo, hi = 0, len(be)
-                while lo < hi:
-                    mid = (lo + hi) // 2
-                    if be[mid] <= t:
-                        lo = mid + 1
-                    else:
-                        hi = mid
-                while lo < len(bs) and t + h > bs[lo]:
-                    t = max(t, be[lo])
-                    lo += 1
+                bs, be, who = busy[eng[i]]
+                lo = hi = len(be)
+                if hi and be[-1] > t:
+                    lo = 0
+                    while lo < hi:
+                        mid = (lo + hi) // 2
+                        if be[mid] <= t:
+                            lo = mid + 1
+                        else:
+                            hi = mid
+                    while lo < len(be) and t + h > bs[lo]:
+                        if be[lo] > t:
+                            t, w = be[lo], -2 - who[lo]
+                        lo += 1
                 bs.insert(lo, t)
                 be.insert(lo, t + h)
+                who.insert(lo, i)
             start[i] = t - off
             end[i] = start[i] + cost[i]
-        return start, end
+            why[i] = w
+        return start, end, why
 
-    def sweep(pri, wait):
-        start, end, rdy = [0.0] * n, [0.0] * n, [0.0] * n
-        left = [len(p) for p in pre]
-        pool = {e: [] for e in "vstgyx"}
-        free = {e: 0.0 for e in "vstgyx"}
+    def forward(key, rounds):
         for i in range(n):
-            if not left[i]:
-                pool[ops[i]["e"]].append(i)
-        for _ in range(n):
-            bt, be = None, None
-            for e, p in pool.items():
-                if p:
-                    t = max(free[e], min([rdy[i] for i in p]))
-                    if bt is None or t < bt:
-                        bt, be = t, e
-            p = pool[be]
-            i = max([k for k in p if rdy[k] <= bt + wait], key=lambda k: pri[k] - (rdy[k] - bt if rdy[k] > bt else 0.0))
-            p.remove(i)
-            start[i] = max(bt, rdy[i])
-            end[i] = start[i] + cost[i]
-            free[be] = start[i] + hold[i]
-            for k, l in post[i]:
-                if end[i] + l > rdy[k]:
-                    rdy[k] = end[i] + l
-                left[k] -= 1
-                if not left[k]:
-                    pool[ops[k]["e"]].append(k)
-        return start, end
+            for j, l in pre[i]:
+                if key[j] > key[i]:
+                    key[i] = key[j]
+        s, e, w = place(sorted(range(n), key=lambda k: (key[k], k)), pre, False)
+        best = (max(e), s, e, w)
+        for _ in range(rounds):
+            s2, e2, w = place(sorted(range(n), key=lambda k: (-e[k], -k)), post, True)
+            s, e, w = place(sorted(range(n), key=lambda k: (-e2[k], k)), pre, False)
+            if max(e) >= best[0]:
+                break
+            best = (max(e), s, e, w)
+        return best
 
-    def polish(start, end):
-        s2, e2 = place(sorted(range(n), key=lambda k: (-end[k], -k)), post, True)
-        return place(sorted(range(n), key=lambda k: (-e2[k], k)), pre, False), e2
+    lvl = [0.0] * n
+    for i in range(n - 1, -1, -1):
+        lvl[i] = cost[i] + max([lvl[k] + l for k, l in post[i]] + [0.0])
+    best = cur = forward([-x for x in lvl], 6)
+    seed = [OPT["seed"]]
 
-    best = None
-    for wait in OPT["wait"]:
-        pri = lvl
-        for _ in range(OPT["passes"]):
-            start, end = sweep([pri[k] + ops[k]["p"] for k in range(n)], wait)
-            (s3, e3), pri = polish(start, end)
-            for s, e in ((start, end), (s3, e3)):
-                if best is None or max(e) < best[0]:
-                    best = (max(e), s, e)
-    start, end = best[1], best[2]
-    order = sorted(range(n), key=lambda k: (start[k], k))
+    def rnd():
+        seed[0] = (seed[0] * 1103515245 + 12345) % 2147483648
+        return seed[0] / 2147483648.0
+
+    for it in range(OPT["tries"]):
+        key = list(cur[1])
+        if rnd() < 0.25:
+            a = rnd() * cur[0]
+            b, amp = a + rnd() * 20000.0, 6000.0 * rnd()
+            c = forward([s + (amp * (rnd() - 0.5) if a <= s <= b else 0.0) for s in key], 2)
+        else:
+            i, arcs = max(range(n), key=lambda k: cur[2][k]), []
+            while cur[3][i] != -1:
+                j = cur[3][i]
+                if j < -1:
+                    j = -2 - j
+                    arcs.append((j, i))
+                i = j
+            for _ in range(1 + int(2 * rnd())):
+                j, i = arcs[int(rnd() * len(arcs))]
+                if rnd() < 0.5:
+                    to, stack = key[j] - 1 - 1500 * rnd() * rnd(), [i]
+                    while stack:
+                        k = stack.pop()
+                        if key[k] > to:
+                            key[k] = to
+                            stack.extend(p for p, l in pre[k])
+                else:
+                    key[j] = key[i] + 1 + 3000 * rnd() * rnd()
+            c = forward(key, int(rnd() < 0.25))
+        if c[0] <= cur[0] - 70.0 * (1 - it / OPT["tries"]) * math.log(1e-9 + rnd()):
+            cur = c
+            if c[0] < best[0]:
+                best = c
+    start, end, order = [0.0] * len(ops), [0.0] * len(ops), []
+    for k in sorted(range(n), key=lambda k: (best[1][k], k)):
+        t = best[1][k]
+        for i in jobs[k][0]:
+            start[i], end[i] = t, t + ops[i]["c"]
+            t = end[i]
+            order.append(i)
     return deps, order, start, end
 
 
@@ -744,7 +850,8 @@ def rank_program(g, core, T, topo):
             g.remote_dma_fused(tr, local_sem=T.sem.left)
             continue
         if m == "dma":
-            q.dma_start(x[0], x[1]).then_inc(T.sem["d%d" % nd], 16)
+            ins = q.dma_start(x[0], x[1], accum_op=ALU.add) if a[2] else q.dma_start(x[0], x[1])
+            ins.then_inc(T.sem["d%d" % nd], 16)
             mark[i] = (T.sem["d%d" % nd], 16)
             nd += 1
             continue
@@ -781,6 +888,8 @@ def rank_program(g, core, T, topo):
                 ins = g.iota(x[0], x[1], x[2], x[3])
             else:
                 ins = g.iota(x[0], x[1], x[2], x[3], allow_small_or_imprecise_dtypes=True)
+        elif m == "asel":
+            ins = g.affine_select(*x)
         else:
             ins = g.partition_broadcast(x[0], x[1], 128)
         if i in wanted:

import math
from concourse.bass import DstId, RemoteDMATransfer
from concourse.mybir import AluOpType as ALU, AxisListType as AX, ActivationFunctionType as AF

N, V, L, RO = 8, 2048, 256, 3
CK = 510 * 32768
OFF = 192.0
FR = 1024.0
UNITS = {(t, k): "CCCC BBBB CCAA AAAA" for t in range(RO) for k in range(2)}
UNITS[(0, 0)] = "CCCC CCCC CCCC CCAA"
OPT = {"xt": ["ssss", "ssss", "svsv"], "pd": 4, "x0": "ssvv", "tries": 4500, "seed": 2, "run": 8, "link": "sss", "xs": "vvv",
       "vn0": "sss", "cc": "sss", "tz": "sss", "dig": "s", "mat": "v", "tf": [4, 4, 4], "at": [4, 4, 4],
       "app": "ss", "nd": "vvv", "vn": "sss", "ek": "iis", "cut": [(0, 8), (8, 16)]}
BOOST = {}
COST = {"cyc": 1.04, "gat": 1.56, "sca": 3.8, "pe": 0.5, "hop": 150.0, "self": 100.0, "dma": 2000.0, "rem": 5000.0}
ESZ = {"b": 2, "f": 4, "i": 4, "u": 2}


def plan():
    ops, phase = [], ["a"]
    top = {"b": 0, "f": 0, "i": 0, "u": 0}

    def new(pool, n):
        al = 64 // ESZ[pool]
        lo = top[pool]
        top[pool] = lo + (n + al - 1) // al * al
        return (pool, lo, lo + n, 1, None, lo)

    def sl(a, lo, hi, step=1, part=None):
        return (a[0], a[1] + lo, a[1] + hi, step, part, a[5])

    def bank(k, lo, hi):
        return ("P%d" % k, lo, hi, 1, None, 0)

    def ind(w, o):
        return ("ind", w, o)

    def cnt(a):
        if a[0] == "ind":
            return 16 * cnt(a[2])
        return (a[2] - a[1] + a[3] - 1) // a[3]

    def isap(a):
        return isinstance(a, tuple)

    def two(a):
        return a[0] in ("b", "u")

    def rec(eng, meth, args, outs, ins, cost):
        rd, wr = [], []
        for a in ins:
            if isap(a):
                rd.extend([a[1], a[2]] if a[0] == "ind" else [a])
        for a in outs:
            if a[0] == "ind":
                wr.append(a[1])
                rd.append(a[2])
            else:
                wr.append(a)
        ops.append({"e": eng, "m": meth, "a": args, "r": rd, "w": wr, "c": cost, "p": BOOST.get(phase[0], 0.0), "ph": phase[0]})

    def vcost(out, a, rate):
        n = cnt(out)
        if out[0] == "ind":
            return 50 + n * COST["sca"] * COST["cyc"]
        if a is not None and a[0] == "ind":
            return 50 + n * COST["gat"] * COST["cyc"]
        return max(64, n * rate) * COST["cyc"]

    def cp(out, a):
        rec("v", "cp", (out, a), [out], [a], vcost(out, a, 0.5 if two(out) and two(a) else 1))

    def tt(out, a, b, op):
        rec("v", "tt", (out, a, b, op), [out], [a, b], vcost(out, a, 1 if "P" in (a[0][0], b[0][0]) else 2))

    def ts(out, a, s1, op0, s2=None, op1=None):
        rec("v", "ts", (out, a, s1, s2, op0, op1), [out], [a, s1, s2], vcost(out, a, 0.5 if two(out) and two(a) else 1))

    def ms(out, c):
        rec("v", "ms", (out, c), [out], [], vcost(out, None, 0.5 if two(out) else 1))

    def red(out, a, op):
        rec("v", "red", (out, a, op), [out], [a], vcost(a, None, 1))

    def scan(out, d0, d1, init, op0, op1):
        rec("v", "scan", (out, d0, d1, init, op0, op1), [out], [d0, d1, init],
            vcost(out, None, 0.5 if two(out) and two(d0) and two(d1) else 1))

    def act(out, a, f, scale=1.0, bias=0.0, acc=None):
        c = 65 + cnt(out) * COST["gat"] * COST["cyc"] if a[0] == "ind" else max(64, cnt(out)) * COST["cyc"]
        rec("s", "act", (out, a, f, scale, bias, acc), [out] + ([acc] if acc else []), [a, scale, bias], c + (20 if acc else 0))

    def mm(out, l, r, start, stop):
        rec("t", "mm", (out, l, r, start, stop), [out], [l, r], max(64, cnt(out)) * COST["pe"] * (4 if l[0] == "f" else 1))

    def iota(out, pat, base=0, cm=0):
        rec("g", "iota", (out, pat, base, cm), [out], [], 130 + 2 * cnt(out) * COST["cyc"])

    def asel(out, a, pat, op, cm, other=0.0):
        rec("g", "asel", (out, a, pat, op, other, 0, cm), [out], [a], 170 + 2 * cnt(out) * COST["cyc"])

    def fill(tb, n, step, base=0):
        for k in range(0, n, 640):
            iota(sl(tb, k, min(n, k + 640)), [[step, min(n, k + 640) - k]], base + step * k)

    def dma(q, out, a, nbytes, adds=False):
        rec(q, "dma", (out, a, adds), [] if out[0] == "hbm" else [out], [] if a[0] == "hbm" else [a],
            COST["dma"] * (1.5 if q == "g" else 1) + nbytes / 250.0)

    def hbm(name, idx=None):
        return ("hbm", name, idx)

    def rows(a, p, n):
        return sl(a, 0, n, 1, slice(p, 128, 16))

    def gat(eng, out, win, off):
        if eng == "v":
            cp(out, ind(win, off))
        else:
            act(out, ind(win, off), AF.Copy)

    def times(eng, out, a, s):
        if eng == "v":
            ts(out, a, s, mul)
        else:
            act(out, a, AF.Copy, s)

    def zr(z, r):
        return sl(z, 15 - r, 143 - r)

    def wrap(out, z, row, n, start=True, stop=True):
        for r in range(16):
            mm(out, zr(z, r), sl(row, r, n, 16), start and r == 0, stop and r == 15)

    add, sub, mul, mx, mn = ALU.add, ALU.subtract, ALU.mult, ALU.max, ALU.min
    band, shr = ALU.bitwise_and, ALU.arith_shift_right
    K0, K1, D0, D1, W, R, Q, U = range(8)

    Z = [new("b", L) for _ in range(RO + 1)]
    X = new("b", V + 2 * L)
    kcol, tcol = new("i", 1), new("i", 1)
    tsi = new("i", 128)
    dma("y", Z[0], hbm("zq"), 65536)
    dma("y", kcol, hbm("kap"), 512)
    dma("y", sl(X, 0, V), hbm("xr"), 524288)
    iota(tcol, [[0, 1]])
    dma("y", rows(tcol, 0, 1), hbm("th"), 32)
    for b in range(4):
        for gm in range(2):
            dma("s", sl(tsi, 32 * b + 16 * gm, 32 * b + 16 * gm + 16),
                hbm("ts", (slice(gm, 8, 2), slice(512 * b, 512 * b + 512))), 8192)

    DIG = new("b", 2560)
    if OPT["dig"] == "s":
        ms(sl(DIG, 0, 320), 0.0)
        for k in (320, 640, 1280):
            act(sl(DIG, k, 2 * k), sl(DIG, 0, k), AF.Copy)
    else:
        ms(sl(DIG, 0, 1280), 0.0)
        act(sl(DIG, 1280, 2560), sl(DIG, 0, 1280), AF.Copy)
    pI, jrow, grow, wrow = new("i", 1), new("b", 143), new("b", 128), new("f", 16)
    iota(pI, [[0, 1]], 0, 1)
    iota(jrow, [[1, 143]])
    iota(sl(wrow, 0, 16, 2), [[1, 8]], 1)
    iota(sl(wrow, 1, 15, 2), [[-1, 7]], 7)
    iota(sl(wrow, 15, 16), [[0, 1]], 1)
    ai, mrow, negk, lw0 = new("i", 160), new("b", L), new("f", L), new("f", 16)
    iota(ai, [[1, 160]], 0, 160)
    iota(grow, [[16, 8], [0, 16]])
    iota(mrow, [[1, 16], [0, 16]])
    iota(negk, [[-1, 16], [0, 16]])
    iota(lw0, [[16, 16]], V, 1)
    g16i, g16, pF, rcol, g15, g160, wcol, rm16, z2c = [new(p, 1) for p in "iffffffff"]
    ts(g16i, pI, 112, band)
    cp(g16, g16i)
    cp(pF, pI)
    tt(rcol, pF, g16, sub)
    ts(g15, g16, 15.0, add)
    ts(g160, g16, 160.0, mul)
    ts(rm16, rcol, -16.0, add)
    m16, t16 = new("f", 16), new("f", 16)
    ts(m16, sl(jrow, 0, 16), rcol, ALU.is_equal)
    tt(t16, m16, wrow, mul)
    red(wcol, t16, add)
    ZW, ZS, ZS2, ZSN, ZN1, ZB, Z4, Z2 = [new("b", 143) for _ in range(8)]
    z1c = new("f", 1)
    ts(ZW, jrow, g15, ALU.is_equal, wcol, mul)
    ts(ZS, jrow, g15, ALU.is_equal, 32768.0, mul)
    times(OPT["mat"], ZS2, ZS, 2.0)
    times(OPT["mat"], ZSN, ZS, -1.0)
    ts(z1c, sl(m16, 0, 1), -1.0, mul)
    ts(ZN1, jrow, g15, ALU.is_equal, z1c, mul)
    ts(ZB, jrow, g15, ALU.is_equal, sl(m16, 1, 2), mul)
    times(OPT["mat"], Z4, ZN1, -4096.0)
    ts(z2c, sl(m16, 1, 2), 4096.0, mul, sl(m16, 0, 1), sub)
    ts(Z2, jrow, g15, ALU.is_equal, z2c, mul)
    I1, NI, IH, INH, I2K, I15, I128, IN80, ICK, I3, N8, BO, BW, DW, TU, TL = [new("b", 128) for _ in range(16)]
    I32, NI32, I32x8 = [new("f", 128) for _ in range(3)]
    crow = sl(jrow, 0, 128)
    zer, zer32 = new("b", 640), new("f", 128)
    iota(sl(zer, 0, 128), [[0, 128]])
    iota(zer32, [[0, 128]])
    ts(I1, crow, pF, ALU.is_equal)
    for t, s in ((NI, -1.0), (I2K, 2048.0), (I32, 1.0)):
        times("s", t, I1, s)
    for t, s in ((ICK, float(-CK)), (I3, 16 * OFF * 32768), (NI32, -1.0), (IH, 0.5), (INH, -0.5), (I15, 1.5), (I128, 128.0),
                 (IN80, -80.0), (N8, -8.0), (I32x8, 8.0)):
        asel(t, zer32 if t[0] == "f" else sl(zer, 0, 128), [[-1, 128]], ALU.not_equal, 1, s)
    ts(BO, grow, g16, ALU.is_equal)
    ts(BW, grow, g16, ALU.is_equal, wcol, mul)
    asel(TU, BO, [[1, 128]], ALU.is_ge, -1)
    asel(TL, BO, [[-1, 128]], ALU.is_gt, 1)
    cidx = new("u", 16)
    ts(cidx, sl(jrow, 0, 16), 0.0, mul, rcol, add)
    BO32, kf, kd, kap, tf0, thc = new("f", 128), new("f", 1), new("f", 16), new("f", 16), new("f", 1), new("f", 1)
    ts(BO32, grow, g16, ALU.is_equal)
    cp(kf, kcol)
    ts(kd, m16, kf, mul)
    mm(bank(U, 0, 16), BO32, kd, True, True)
    act(kap, bank(U, 0, 16), AF.Copy)
    cp(tf0, tcol)
    mm(bank(U, 0, 1), BO32, tf0, True, True)
    act(thc, bank(U, 0, 1), AF.Copy)
    LW, LD, LE = new("f", 16), new("f", 16), new("f", 16)
    ts(LW, lw0, g16, sub)
    ts(LD, LW, 256.0, add)
    ts(LE, LW, 255.0, add)
    ones, noff, c4k, c16, gap = new("b", L), new("b", L), new("b", 16), new("b", 128), new("b", 160)
    iota(ones, [[0, L]], 1)
    iota(noff, [[0, L]], -int(OFF))
    iota(c4k, [[0, 16]], 4096)
    iota(c16, [[0, 128]], 16)
    iota(gap, [[0, 160]], -256)
    iota(sl(zer, 128, 640), [[0, 512]])
    half, thr, big0, big, pw16, pcol = new("b", L), new("b", L), new("f", 1), new("f", 1), new("f", 16), new("f", 1)
    ms(half, 0.5)
    ms(sl(half, 0, L, 16), 1.0)
    ms(big0, 2.0 ** 60)
    ts(big, big0, 2.0 ** 61, mul)
    scan(thr, half, sl(zer, 0, L), big, mul, mx)
    tt(pw16, sl(thr, 0, 16), m16, mul)
    red(big0, pw16, add)
    ts(pcol, big0, 2.0 ** -50, mul, 2.0 ** -50, mul)
    ts(DW, grow, g16, ALU.is_equal, pcol, mul)

    ab, loi, hii, lo, hi = new("i", 160), new("i", 160), new("i", 160), new("b", 160), new("b", 160)
    ts(ab, ai, g160, sub)
    ts(loi, ab, 15, band)
    ts(hii, ab, 4, shr)
    ts(lo, loi, 1 / FR, mul)
    ts(hi, hii, 2 / FR, mul)
    dma("y", rows(DIG, 0, 2560), lo, 40960)
    dma("y", rows(DIG, 14, 2560), hi, 40960)
    XT = [new("f", 2560), new("f", 2560)]
    dma("g", sl(XT[1], 0, V), hbm("xr"), 1048576)
    for p in (0, 14):
        dma("g", rows(XT[1], p, V), rows(DIG, p, V), 65536, True)
    G = [new("b", 2560) for _ in range(RO)]
    M = [new("b", 2560) for _ in range(RO)]
    CU = [new("b", 2560) for _ in range(RO)]
    GW = [2560, 2320, 2320]
    IOT, TS = new("f", V), new("f", V)
    for t in range(RO):
        fill(G[t], GW[t], 0)
        dma("y", rows(G[t], 1, GW[t]), sl(gap, 0, GW[t] // 16), 16 * GW[t])
        fill(M[t], V, 0)
    fill(IOT, V, 1)
    tsf, tst, tsw = new("f", 128), new("f", 128), new("u", 128)
    cp(tsf, tsi)
    rec("v", "tr", (tst, tsf), [tst], [tsf], 128 * COST["cyc"])
    cp(tsw, tst)
    PD = new("b", V + L)
    phase[0] = "b"
    n = 128 // OPT["pd"]
    for k in range(0, 128, n):
        cp(ind(sl(PD, 0, V), sl(tsw, k, k + n)), sl(DIG, 16 * k, 16 * (k + n)))
    phase[0] = "c"
    n = 128 // len(OPT["x0"])
    for k, e in enumerate(OPT["x0"]):
        o, a = sl(XT[0], 16 * n * k, 16 * n * (k + 1)), ind(sl(XT[1], 0, V), sl(tsw, n * k, n * (k + 1)))
        if e == "v":
            ts(o, a, OFF, add)
        else:
            act(o, a, AF.Identity, 1.0, OFF)

    def regather(out, win, off, engs):
        n = 128 // len(engs)
        for k, e in enumerate(engs):
            gat(e, sl(out, 16 * n * k, 16 * n * (k + 1)), win, sl(off, n * k, n * (k + 1)))

    colA, thA, thK = new("f", 1), new("f", 1), new("f", 1)
    ms(colA, -13.0)
    thB, thL = new("f", 1), new("f", 1)
    ts(thA, thc, 0.5, add)
    ts(thK, thc, -509.0, add, 32768.0, mul)
    ts(thB, thc, 128.5, add)
    ts(thL, thc, 128.0 - 509.0, add, 32768.0, mul)

    DT, AB = new("b", 16 * L), new("b", 16 * L)
    EQ = [new("b", 2176), new("b", 2176)]
    dbank = [0]

    def nearest(units, win, off, zrow, low, nodes):
        o0 = OFF if nodes else 0.0
        acc, groups, lo = None, [], 0
        for part in units.split():
            groups.append((lo, lo + len(part)))
            lo += len(part)
        units = "".join(units.split())
        for gi, (lo, hi) in enumerate(groups):
            m = lo
            while m < hi:
                e = m
                while e < hi and units[e] == units[m] and e - m < 2:
                    e += 1
                d, a = sl(DT, L * m, L * e), sl(AB, L * m, L * e)
                if units[m] == "C":
                    gat("s", d, win, sl(off, 16 * m, 16 * e))
                    bk = (D0, D1)[dbank[0] & 1]
                    dbank[0] += 1
                    for j in range(m, e):
                        o = bank(bk, L * (j - m), L * (j - m + 1))
                        mm(o, NI, zrow, True, False)
                        mm(o, I1, sl(DT, L * j, L * j + L), False, True)
                    act(a, bank(bk, 0, L * (e - m)), AF.Abs, 1.0, -o0)
                else:
                    for j in range(m, e):
                        tt(sl(DT, L * j, L * j + L), ind(win, sl(off, 16 * j, 16 * j + 16)), zrow, sub)
                    if units[m] == "A":
                        act(a, d, AF.Abs, 1.0, -o0)
                    else:
                        ts(a, d, o0, mx, -o0, add)
                m = e
            bk = (K0, K1)[gi & 1]
            w = 16 * (hi - lo)
            whole = bank(bk, 0, w)
            if nodes:
                mm(whole, I2K, sl(ones, 0, w), True, False)
                mm(whole, ICK, sl(ones, 0, w), False, False)
            else:
                mm(whole, I2K, sl(mrow, 16 * lo, 16 * hi), True, False)
            last = "B" in units[lo:hi]
            il = NI32 if nodes else I32
            if not last:
                mm(whole, il, sl(low, 16 * lo, 16 * hi), False, False)
            m = lo
            while m < hi:
                e = m
                while e < hi and (units[e] == "B") == (units[m] == "B"):
                    e += 1
                o = bank(bk, 16 * (m - lo), 16 * (e - lo))
                if units[m] == "B":
                    if nodes:
                        mm(o, I3, sl(ones, 0, 16 * (e - m)), False, False)
                    for r in range(16):
                        mm(o, zr(ZSN, r), sl(DT, L * m + r, L * e, 16), False, False)
                for r in range(16):
                    mm(o, zr(ZS2 if units[m] == "B" else ZS, r), sl(AB, L * m + r, L * e, 16), False, e == hi and r == 15 and not last)
                m = e
            if last:
                mm(whole, il, sl(low, 16 * lo, 16 * hi), False, True)
            nxt = new("i" if w == 16 and hi == 16 else "f", w)
            if acc is None:
                act(nxt, whole, AF.Copy)
            else:
                tt(nxt, whole, acc, mn)
            acc = nxt
            goal = 16 * (groups[gi + 1][1] - hi) if hi < 16 else 16
            while w > goal:
                w //= 2
                nxt = new("i" if w == 16 and hi == 16 else "f", w)
                tt(nxt, sl(acc, 0, w), sl(acc, w, 2 * w), mn)
                acc = nxt
        return acc

    def firsts(dig, kw, miss, eq, bk, spare, flag=None):
        kr, km, fr, fw = new("u", L), new("f", 16), new("b", L), new("f", 16)
        mm(bank(Q, 256, 512), BW, dig, True, True)
        ts(kr, bank(Q, 256, 512), FR, mul)
        tt(km, kw, miss, add)
        mm(bank(Q, 0, L), NI, thr, True, False)
        o = 0
        for c in range(16):
            n = L - 16 * c
            ts(sl(eq, o, o + n), sl(kr, 16 * c, L), sl(km, c, c + 1), ALU.is_equal, 2.0 ** (99 - 15 * c), mul)
            mm(bank(Q, 16 * c, L), DW, sl(eq, o, o + n), False, c == 15)
            o += n
        act(fr, bank(Q, 0, L), AF.Sign)
        y = bank(bk, 0, 16)
        mm(y, I1, c4k, True, False)
        mm(y, I1, miss, False, False)
        if flag:
            wrap(y, flag[0], flag[1], L, False, False)
        wrap(y, Z4, fr, L, False)
        tt(fw, y, spare, mn)
        return fw

    ci, hi_, tf, h32 = new("i", L), new("i", L), new("f", L), new("f", L)
    atf, tg = new("f", L), new("f", L)
    for t in range(RO):
        z, xt, final = Z[t], sl(XT[t & 1], 0, V), t + 1 == RO
        phase[0] = "h%d" % t
        u2, sq, a2, hu = new("f", 16), new("f", 16), new("i", 16), new("u", L)
        wrap(bank(W, 0, 16), ZW, z, L)
        cp(u2, bank(W, 0, 16))
        tt(sq, bank(W, 0, 16), u2, mul)
        ts(a2, sq, colA, add, 1.0 / 32, mul)
        for lo, hi in OPT["cut"]:
            a, b = 16 * lo, 16 * hi
            for m in range(lo, hi):
                times("v" if m < OPT["tf"][t] else "s", sl(tf, 16 * m, 16 * m + 16), u2, sl(kap, m, m + 1))
            tt(sl(ci, a, b), ind(a2, sl(cidx, lo, hi)), sl(tf, a, b), add)
            ts(sl(hi_, a, b), sl(ci, a, b), V - 1, band)
            cp(sl(hu, a, b), sl(hi_, a, b))
            ts(sl(h32, a, b), sl(hi_, a, b), float(-CK), add)
        phase[0] = "s%d" % t
        key = nearest(UNITS[(t, 0)], sl(X, 0, V), hu, z, h32, False)
        si, su = new("i", 16), new("u", 16)
        ts(si, key, V - 1, band)
        cp(su, si)
        phase[0] = "m%d" % t
        xp = new("b", 2 * L)
        xs, pd = sl(xp, 0, L), sl(xp, L, 2 * L)
        gat(OPT["xs"][t], xs, sl(X, 0, V), su)
        gat("s", pd, sl(PD, 0, V), su)
        wrap(bank(W, 0, 32), ZW, xp, 2 * L)
        i2, dm, d2, au = new("i", 16), new("i", 16), new("f", 16), new("u", L)
        tau = p = new("f", 16)
        pu = new("u", 16)
        if t:
            ts(pu, bank(W, 16, 32), FR, mul)
        cp(i2, bank(W, 0, 16))
        ts(tau, bank(W, 16, 32), FR, mul)
        for k in range(t):
            cg, p2 = new("b", L), new("f", 16)
            gat(OPT["link"][t + k - 1], cg, sl(CU[k], 0, GW[k]), pu)
            mm(bank(W, 0, 16), I32, p, True, False)
            wrap(bank(W, 0, 16), ZN1, cg, L, False)
            if k + 1 < t:
                pu = new("u", 16)
                cp(pu, bank(W, 0, 16))
            cp(p2, bank(W, 0, 16))
            p = p2
        ts(dm, i2, 15, band)
        ts(d2, dm, 1.0, add)
        for c in range(16 if OPT["at"][t] >= 0 else 0):
            o, ks, dc, pc = sl(atf, c, L, 16), sl(negk, 0, L, 16), sl(d2, c, c + 1), sl(p, c, c + 1)
            if c < OPT["at"][t]:
                ts(o, ks, dc, mul, pc, add)
            else:
                act(o, ks, AF.Identity, dc, pc)
        for lo, hi in OPT["cut"]:
            a, b = 16 * lo, 16 * hi
            if OPT["at"][t] < 0:
                if lo and OPT["at"][t] == -2:
                    for m in range(lo, hi):
                        act(sl(tg, 16 * m, 16 * m + 16), d2, AF.Copy, float(-m))
                else:
                    tt(sl(tg, a, b), ind(d2, sl(cidx, lo, hi)), sl(negk, a, b), mul)
                tt(sl(atf, a, b), ind(p, sl(cidx, lo, hi)), sl(tg, a, b), add)
            ts(sl(au, a, b), sl(atf, a, b), -1.0, add)
        phase[0] = "p%d" % t
        miss = new("b", 16)
        ts(miss, key, thK, ALU.is_ge, 8192.0, mul)
        adz, sgn, cc, dz, vs = [new("b", L) for _ in range(5)]
        mm(bank(U, 0, L), I1, z, True, False)
        mm(bank(U, 0, L), NI, xs, False, True)
        act(adz, bank(U, 0, L), AF.Abs)
        if OPT["cc"][t] == "s":
            act(dz, bank(U, 0, L), AF.Copy)
            ts(cc, dz, -2.0, mx, 2.0, mn)
        else:
            ts(cc, bank(U, 0, L), -2.0, mx, 2.0, mn)
        mm(bank(U, L, 2 * L), BO, adz, True, True)
        nsum = new("f", 1)
        act(sgn, bank(U, L, 2 * L), AF.Sign, -1.0, thA, None if final else nsum)
        mm(bank(U, 0, L), IH, z, True, False)
        mm(bank(U, 0, L), IH, xs, False, True)
        act(vs, bank(U, 0, L), AF.Identity, 1.0, OFF - 0.25)
        if not final:
            colA, thA, thK = new("f", 1), new("f", 1), new("f", 1)
            act(colA, nsum, AF.Identity, -16.0, 4083.0)
            act(thA, nsum, AF.Identity, -0.5, thB)
            act(thK, nsum, AF.Identity, -16384.0, thL)
        else:
            phase[0] = "k"
            cf, cr, ids = new("f", 256), new("b", 256), new("f", 128)
            dma("y", sl(cf, 0, 128), rows(xt, 0, V), 65536)
            dma("y", sl(cf, 128, 256), rows(xt, 14, V), 65536)
            act(cr, cf, AF.Copy)
            mm(bank(U, 0, 128), I32, sl(cf, 0, 128), True, False)
            mm(bank(U, 0, 128), I32x8, sl(cf, 128, 256), False, False)
            mm(bank(U, 0, 128), NI, sl(cr, 0, 128), False, False)
            mm(bank(U, 0, 128), N8, sl(cr, 128, 256), False, True)
            act(ids, bank(U, 0, 128), AF.Copy, FR)
            dma("y", rows(XT[1 - (t & 1)], 0, V), ids, 65536)
        phase[0] = "d%d" % t
        q32, uu = new("f", 32), new("u", 48)
        fs = firsts(pd, tau, miss, EQ[0], U, LW)
        tt(sl(q32, 0, 16), fs, si, mx)
        tt(sl(q32, 16, 32), fs, p, mx)
        q, sou, qu = sl(q32, 16, 32), sl(uu, 0, 16), sl(uu, 16, 48)
        cp(sl(uu, 0, 32), q32)
        ts(sl(uu, 32, 48), q, 1.0, add)
        phase[0] = "x%d" % t
        tt(ind(X, sou), vs, noff, add)
        if final:
            gat("s", sl(XT[1 - (t & 1)], V, V + L), IOT, su)
        else:
            if OPT["app"][t] == "v":
                tt(sl(XT[t & 1], V, V + L), ind(sl(DIG, 0, V), su), vs, add)
            else:
                sd = new("b", L)
                gat("s", sd, sl(DIG, 0, V), su)
                mm(bank(U, 0, L), I1, vs, True, False)
                mm(bank(U, 0, L), I1, sd, False, True)
                act(sl(XT[t & 1], V, V + L), bank(U, 0, L), AF.Copy)
            cp(ind(PD, sou), sl(DIG, V + L * t, V + L * t + L))
        phase[0] = "o%d" % t
        gw = GW[t]
        cp(ind(sl(G[t], 0, V + L), sl(qu, 0, 16)), ones)
        for k in range(0, gw, 640):
            e = min(gw, k + 640)
            scan(sl(CU[t], k, e), sl(G[t], k, e), sl(zer, 0, e - k), 0.0 if k == 0 else sl(CU[t], k - 1, k), add, mx)
        cg, ps, pu, dw, of, ou = new("b", 2 * L), new("f", 16), new("u", 16), new("b", 128), new("f", 128), new("u", 128)
        gat("s", cg, sl(CU[t], 0, gw), qu)
        mm(bank(U, 0, 16), I32, q, True, False)
        wrap(bank(U, 0, 16), Z2, sl(cg, L, 2 * L), L, False)
        tt(ps, bank(U, 0, 16), LE, mn)
        ts(pu, ps, 1.0, add)
        cp(ind(M[t], pu), sl(cg, 0, L))
        wrap(bank(U, 0, 128), ZB, M[t], V)
        act(dw, bank(U, 0, 128), AF.Copy)
        mm(bank(U, 0, 128), TU, dw, True, False)
        mm(bank(U, 1, 128), TL, sl(dw, 0, 127), False, True)
        scan(of, bank(U, 0, 128), c16, rm16, add, add)
        cp(ou, of)
        if final:
            phase[0] = "t"
            regather(TS, sl(XT[1 - (t & 1)], 0, V + L), ou, OPT["xt"][t])
            for k in (0, V // 2):
                dma("y", hbm("yt", (slice(0, 8), slice(k, k + V // 2))), rows(sl(TS, k, k + V // 2), 0, V // 2), 32768)
        phase[0] = "n%d" % t
        keyn = nearest(UNITS[(t, 1)], xt, au, xs, atf, True)
        ni, nu = new("i", 16), new("u", 16)
        ts(ni, keyn, 4095, band)
        ts(nu, ni, -1.0, mul, 2047.0, add)
        phase[0] = "z%d" % t
        xn, tz, zs = new("b", L), new("b", L), new("b", L)
        mm(bank(W, 0, L), INH, z, True, False)
        mm(bank(W, 0, L), I128, sgn, False, False)
        mm(bank(R, 0, L), I1, z, True, False)
        mm(bank(R, 0, L), IN80, sgn, False, False)
        gat(OPT["vn0"][t], xn, xt, nu)
        mm(bank(W, 0, L), I15, xn, False, True)
        mm(bank(R, 0, L), NI, xn, False, False)
        if OPT["tz"][t] == "v":
            ts(tz, bank(W, 0, L), 31.75 - 1.5 * OFF, add, 0.0, mx)
        else:
            act(tz, bank(W, 0, L), AF.Relu, 1.0, 31.75 - 1.5 * OFF)
        mm(bank(R, 0, L), I1, tz, False, True)
        act(zs, bank(R, 0, L), AF.Abs, 1.0, OFF - 80.0)
        rec("g", "send", (t, zs, Z[t + 1]), [], [zs], 600)
        rec("s", "own", (t, zs, Z[t + 1]), [Z[t + 1]], [zs], 64)
        rec("x", "arr", (t, len(ops) - 2), [Z[t + 1]], [], COST["rem"])
        phase[0] = "e%d" % t
        nd, nw, vn, ng, qn, un = new("b", L), new("f", 16), new("b", L), new("b", L), new("f", 32), new("u", 32)
        if OPT["nd"][t] == "v":
            tt(nd, ind(xt, nu), xn, sub)
        else:
            wn = new("f", L)
            gat("s", wn, xt, nu)
            mm(bank(R, 0, L), NI, xn, True, False)
            mm(bank(R, 0, L), I32, wn, False, True)
            act(nd, bank(R, 0, L), AF.Copy)
        gat("s", ng, sl(G[t] if final else CU[t], 0, V), nu)
        wrap(bank(W, 0, 16), ZW, nd, L)
        act(nw, bank(W, 0, 16), AF.Copy, FR)
        nf, n2, keys = new("f", 16), new("f", 16), (nd, nw)
        if not final or OPT["ek"][t] != "i":
            cp(nf, nu)
        if OPT["ek"][t] != "i":
            keys = (new("b", L), nf)
            gat(OPT["ek"][t], keys[0], sl(DIG, 0, V), nu)
        fn = firsts(keys[0], keys[1], miss, EQ[1], W, LD, (Z4 if final else Z2, ng))
        if not final:
            tt(n2, bank(W, 0, 16), nf, add)
            tt(sl(qn, 16, 32), n2, LD, mn)
        tt(sl(qn, 0, 16), fn, nw, mx)
        mm(bank(R, 0, L), I1, cc, True, False)
        mm(bank(R, 0, L), I1, xn, False, True)
        if OPT["vn"][t] == "v":
            ts(vn, bank(R, 0, L), OFF, mx, OFF + 63.0, mn)
        else:
            v1 = new("b", L)
            act(v1, bank(R, 0, L), AF.Relu, 1.0, -OFF)
            ts(vn, v1, 63.0, mn, OFF, add)
        cp(sl(un, 0, 16), sl(qn, 0, 16))
        tt(ind(X, sl(un, 0, 16)), vn, noff, add)
        if not final:
            phase[0] = "r%d" % t
            vx = new("f", L)
            regather(XT[(t + 1) & 1], sl(XT[t & 1], 0, V + L), ou, OPT["xt"][t])
            mm(bank(R, 0, L), I1, vn, True, False)
            mm(bank(R, 0, L), I1, nd, False, True)
            act(vx, bank(R, 0, L), AF.Copy)
            cp(sl(un, 16, 32), sl(qn, 16, 32))
            cp(ind(XT[(t + 1) & 1], sl(un, 16, 32)), vx)
    dma("y", hbm("yx"), sl(X, 0, V), 524288)
    dma("s", hbm("yz"), Z[RO], 65536)
    return ops, top


def depend(ops):
    hist = {}
    deps = []
    for i, o in enumerate(ops):
        d = set()
        if o["m"] == "arr":
            d.add(o["a"][1])
        for aps, isw in ((o["r"], False), (o["w"], True)):
            for a in aps:
                if a[0][0] == "P":
                    lo, hi, w = 0, 512, True
                else:
                    lo, hi, w = a[1], a[2], isw
                h = hist.setdefault((a[0], a[5]), [])
                keep = []
                for e in h:
                    hitx = e[0] < hi and lo < e[1] and (a[4] is None or e[4] is None or a[4].start == e[4].start)
                    if a[3] == e[5] and (lo - e[0]) % a[3]:
                        hitx = False
                    if hitx and (w or e[2]) and e[3] != i and not (o["m"] == "arr" and ops[e[3]]["m"] == "own"):
                        d.add(e[3])
                    if not (w and lo <= e[0] and e[1] <= hi and o["m"] != "arr" and a[4] is None and a[3] == 1):
                        keep.append(e)
                keep.append((lo, hi, w, i, a[4], a[3]))
                hist[(a[0], a[5])] = keep
        deps.append(d)
    return deps


def schedule(ops, deps=None):
    deps = depend(ops) if deps is None else deps
    job, jobs = [0] * len(ops), []
    for i, o in enumerate(ops):
        if o["e"] == "t" and ops[i - 1]["e"] == "t" and o["a"][0][0] == ops[i - 1]["a"][0][0] and len(jobs[-1][0]) < OPT["run"] and \
                all(job[j] == job[i - 1] or job[j] in jobs[-1][1] for j in deps[i]):
            jobs[-1][0].append(i)
        else:
            jobs.append(([i], {job[j] for j in deps[i]}))
        job[i] = len(jobs) - 1
    n = len(jobs)
    eng = [ops[m[0]]["e"] for m, d in jobs]
    kind = [ops[m[0]]["m"] for m, d in jobs]
    cost = [sum(ops[i]["c"] for i in m) for m, d in jobs]
    hold = [(1000.0 if eng[k] == "g" else 60.0) if kind[k] == "dma" else (0.0 if kind[k] == "arr" else cost[k]) for k in range(n)]

    def lag(j, i):
        if eng[j] == eng[i] and kind[j] != "dma":
            return 0.0 if eng[i] == "t" else COST["self"]
        return COST["hop"]

    pre = [[(j, lag(j, i)) for j in jobs[i][1]] for i in range(n)]
    post = [[] for _ in range(n)]
    for i in range(n):
        for j, l in pre[i]:
            post[j].append((i, l))

    def place(seq, before, back):
        busy = {e: ([], [], []) for e in "vstgyx"}
        start, end, why = [0.0] * n, [0.0] * n, [-1] * n
        for i in seq:
            t, w = 0.0, -1
            for j, l in before[i]:
                if end[j] + l > t:
                    t, w = end[j] + l, j
            off = cost[i] - hold[i] if back else 0.0
            t += off
            h = hold[i]
            if h:
                bs, be, who = busy[eng[i]]
                lo = hi = len(be)
                if hi and be[-1] > t:
                    lo = 0
                    while lo < hi:
                        mid = (lo + hi) // 2
                        if be[mid] <= t:
                            lo = mid + 1
                        else:
                            hi = mid
                    while lo < len(be) and t + h > bs[lo]:
                        if be[lo] > t:
                            t, w = be[lo], -2 - who[lo]
                        lo += 1
                bs.insert(lo, t)
                be.insert(lo, t + h)
                who.insert(lo, i)
            start[i] = t - off
            end[i] = start[i] + cost[i]
            why[i] = w
        return start, end, why

    def forward(key, rounds):
        for i in range(n):
            for j, l in pre[i]:
                if key[j] > key[i]:
                    key[i] = key[j]
        s, e, w = place(sorted(range(n), key=lambda k: (key[k], k)), pre, False)
        best = (max(e), s, e, w)
        for _ in range(rounds):
            s2, e2, w = place(sorted(range(n), key=lambda k: (-e[k], -k)), post, True)
            s, e, w = place(sorted(range(n), key=lambda k: (-e2[k], k)), pre, False)
            if max(e) >= best[0]:
                break
            best = (max(e), s, e, w)
        return best

    lvl = [0.0] * n
    for i in range(n - 1, -1, -1):
        lvl[i] = cost[i] + max([lvl[k] + l for k, l in post[i]] + [0.0])
    best = cur = forward([-x for x in lvl], 6)
    seed = [OPT["seed"]]

    def rnd():
        seed[0] = (seed[0] * 1103515245 + 12345) % 2147483648
        return seed[0] / 2147483648.0

    for it in range(OPT["tries"]):
        key = list(cur[1])
        if rnd() < 0.25:
            a = rnd() * cur[0]
            b, amp = a + rnd() * 20000.0, 6000.0 * rnd()
            c = forward([s + (amp * (rnd() - 0.5) if a <= s <= b else 0.0) for s in key], 2)
        else:
            i, arcs = max(range(n), key=lambda k: cur[2][k]), []
            while cur[3][i] != -1:
                j = cur[3][i]
                if j < -1:
                    j = -2 - j
                    arcs.append((j, i))
                i = j
            for _ in range(1 + int(2 * rnd())):
                j, i = arcs[int(rnd() * len(arcs))]
                if rnd() < 0.5:
                    to, stack = key[j] - 1 - 1500 * rnd() * rnd(), [i]
                    while stack:
                        k = stack.pop()
                        if key[k] > to:
                            key[k] = to
                            stack.extend(p for p, l in pre[k])
                else:
                    key[j] = key[i] + 1 + 3000 * rnd() * rnd()
            c = forward(key, int(rnd() < 0.25))
        if c[0] <= cur[0] - 70.0 * (1 - it / OPT["tries"]) * math.log(1e-9 + rnd()):
            cur = c
            if c[0] < best[0]:
                best = c
    start, end, order = [0.0] * len(ops), [0.0] * len(ops), []
    for k in sorted(range(n), key=lambda k: (best[1][k], k)):
        t = best[1][k]
        for i in jobs[k][0]:
            start[i], end[i] = t, t + ops[i]["c"]
            t = end[i]
            order.append(i)
    return deps, order, start, end


OPS, TOP = plan()
DEPS, ORDER, START, END = schedule(OPS)
NDMA = sum(1 for o in OPS if o["m"] == "dma")
SCRATCH = {"b": ("sbuf", [128, TOP["b"]], "bfloat16"), "f": ("sbuf", [128, TOP["f"]], "float32"),
           "i": ("sbuf", [128, TOP["i"]], "int32"), "u": ("sbuf", [128, TOP["u"]], "uint16")}
for _k in range(8):
    SCRATCH["P%d" % _k] = ("psum", [128, 512], "float32")
SEMAPHORES = ["qv", "qs", "qt", "qg", "left"] + ["arr%d" % _k for _k in range(RO)] + ["d%d" % _k for _k in range(NDMA)]


def routes(T, topo, src):
    dsts = [c for c in T.cores if c != src]
    dsts.sort(key=lambda c: (len(topo.engines(src, c)), (T.rank_of(c) - T.rank_of(src)) % N))
    used, out = set(), []
    for k, c in enumerate(dsts):
        can = topo.engines(src, c)
        free = [e for e in can if e not in used]
        alike = sum(1 for x in dsts[k:] if topo.engines(src, x) == can)
        w = 1
        while 2 * w * alike <= len(free):
            w *= 2
        take = free[:w]
        used.update(take)
        out.append((T.rank_of(c), take))
    return out


def rank_program(g, core, T, topo):
    rank = T.rank_of(core)
    if rank is None:
        return
    B = L // N
    queue = {"v": g.vector, "s": g.scalar, "t": g.tensor, "g": g, "y": g.sync}
    mine = routes(T, topo, core)
    expect = sum(len(e) for c in T.cores if c != core for r, e in routes(T, topo, c) if r == rank)

    def ap(a):
        if not isinstance(a, tuple):
            return a
        if a[0] == "ind":
            return ap(a[1]).indirect(ap(a[2]))
        if a[0] == "hbm":
            return T[a[1]][:] if a[2] is None else T[a[1]][a[2]]
        part = slice(0, 128) if a[4] is None else a[4]
        return T[a[0]][part, a[1]:a[2]] if a[3] == 1 else T[a[0]][part, a[1]:a[2]:a[3]]

    def needs(i):
        return [j for j in DEPS[i] if not (OPS[j]["e"] == "t" and OPS[i]["e"] == "t") and OPS[i]["m"] != "arr"]

    pos = {i: k for k, i in enumerate(ORDER)}
    seen, wanted, waits = {}, set(), {}
    for i in ORDER:
        e, w = OPS[i]["e"], {}
        for j in needs(i):
            key = j if OPS[j]["m"] in ("dma", "arr") else OPS[j]["e"]
            if pos[j] > seen.get((e, key), -1) and (key not in w or pos[j] > pos[w[key]]):
                w[key] = j
        for key, j in w.items():
            seen[(e, key)] = pos[j]
            wanted.add(j)
        waits[i] = list(w.values())
    mark, count, nd, left = {}, {e: 0 for e in "vstg"}, 0, 0
    for i in ORDER:
        o = OPS[i]
        e, m, a = o["e"], o["m"], o["a"]
        if m == "arr":
            mark[i] = (T.sem["arr%d" % a[0]], expect)
            continue
        q = queue[e]
        for j in waits[i]:
            q.wait_ge(mark[j][0], mark[j][1])
        x = [ap(y) for y in a]
        if m == "send":
            tr = []
            for r, eng in mine:
                rid, pid = topo.addr(T.cores[r], core)
                tr.append(RemoteDMATransfer(
                    dst_ids=[DstId(rid=rid, pnc=pid)], dma_engine_mask=sum(1 << k for k in eng),
                    remote_sem=T.sem["arr%d" % a[0]], src=T.b[:, a[1][1] + B * r:a[1][1] + B * r + B],
                    dst=T.b[:, a[2][1] + B * rank:a[2][1] + B * rank + B]))
                left += len(eng)
            g.remote_dma_fused(tr, local_sem=T.sem.left)
            continue
        if m == "dma":
            ins = q.dma_start(x[0], x[1], accum_op=ALU.add) if a[2] else q.dma_start(x[0], x[1])
            ins.then_inc(T.sem["d%d" % nd], 16)
            mark[i] = (T.sem["d%d" % nd], 16)
            nd += 1
            continue
        if m == "cp":
            ins = q.tensor_copy(x[0], x[1])
        elif m == "tt":
            ins = q.tensor_tensor(x[0], x[1], x[2], x[3])
        elif m == "ts":
            ins = q.tensor_scalar(x[0], x[1], x[2], None, x[4]) if x[5] is None else q.tensor_scalar(*x)
        elif m == "ms":
            ins = q.memset(x[0], x[1])
        elif m == "red":
            ins = q.tensor_reduce(x[0], x[1], AX.X, x[2])
        elif m == "scan":
            ins = q.tensor_tensor_scan(*x)
        elif m == "tr":
            ins = q.transpose(x[0], x[1])
        elif m == "act":
            kw = {}
            if a[3] != 1.0:
                kw["scale"] = x[3]
            if a[4] != 0.0:
                kw["bias"] = x[4]
            if a[5] is not None:
                kw["accum_out"] = x[5]
            ins = q.activation(x[0], x[1], x[2], **kw)
        elif m == "own":
            ins = q.activation(T.b[:, a[2][1] + B * rank:a[2][1] + B * rank + B],
                               T.b[:, a[1][1] + B * rank:a[1][1] + B * rank + B], AF.Copy)
        elif m == "mm":
            ins = q.matmul(*x)
        elif m == "iota":
            if a[0][0] == "i":
                ins = g.iota(x[0], x[1], x[2], x[3])
            else:
                ins = g.iota(x[0], x[1], x[2], x[3], allow_small_or_imprecise_dtypes=True)
        elif m == "asel":
            ins = g.affine_select(*x)
        else:
            ins = g.partition_broadcast(x[0], x[1], 128)
        if i in wanted:
            count[e] += 1
            ins.then_inc(T.sem["q" + e], 1)
            mark[i] = (T.sem["q" + e], count[e])
    for i in ORDER:
        if OPS[i]["m"] == "dma" and i not in wanted:
            g.wait_ge(mark[i][0], 16)
    g.wait_ge(T.sem.left, left)
